import numpy as np
import ml_dtypes


def mxq(x, axis, fmt="e4m3"):
    dtype, down = {"e4m3": (ml_dtypes.float8_e4m3fn, 7), "e5m2": (ml_dtypes.float8_e5m2, 14)}[fmt]
    v = np.moveaxis(np.asarray(x, np.float32).astype(ml_dtypes.bfloat16).astype(np.float64), axis, -1)
    blocks = v.reshape(v.shape[:-1] + (-1, 32))
    amax = np.abs(blocks).max(-1, keepdims=True)
    byte = np.maximum(np.where(amax > 0, np.frexp(amax)[1] - 1 + 127, 0) - down, 1)
    scale = np.exp2(byte - 127.0)
    codes = (blocks / scale).astype(np.float32).astype(dtype).astype(np.float64)
    return np.moveaxis((codes * scale).reshape(v.shape), -1, axis)


WIDE = False


def mx_kscale(k):
    if not WIDE:
        return np.ones(k)
    levels = np.array([10, -10, 5, -5, 0])
    if k % 512:
        return np.exp2(np.random.permutation(np.resize(levels, k // 32))).repeat(32)
    a = np.empty((k // 512, 16))
    for p in range(k // 512):
        a[p, :8] = np.random.permutation(np.resize(levels, 8))
        for g in range(8):
            far = levels[np.abs(levels - a[p, g]) >= 10]
            a[p, g + 8] = far[np.random.randint(len(far))]
    return np.exp2(a.ravel()).repeat(32)


def f64(x):
    return np.asarray(x).astype(np.float64)


def striped(idx):
    return np.tile(idx.reshape(-1, 16).T, (8, 1)).astype(np.uint16)


def unstriped(offs):
    return offs[:16].T.reshape(-1).astype(np.int64)


def striped8(idx):
    return np.concatenate([x.reshape(-1, 16).T for x in idx]).astype(np.uint16)


def runs(offs, k):
    lists = np.stack([offs[16 * r : 16 * r + 16].T.reshape(-1) for r in range(8)]).astype(np.int64)
    return lists[np.arange(k) % 512 // 64]


def pack_weight(w):
    k, n = w.shape
    w = f64(np.asarray(w, np.float32).astype(ml_dtypes.bfloat16)).reshape(k // 32, 32, n)
    amax = np.abs(w).max(1)
    byte = np.clip(np.where(amax > 0, np.frexp(amax)[1] - 1 + 127 - 7, 1), 1, 254)
    scaled = (w * np.exp2(127.0 - byte)[:, None, :]).reshape(k, n).astype(np.float32)
    words = np.ascontiguousarray(scaled.reshape(k // 512, 128, 4, n).transpose(0, 1, 3, 2)).astype(ml_dtypes.float8_e4m3fn).view(np.uint8)
    return words, np.ascontiguousarray(byte.astype(np.uint8).reshape(k // 512, 16, n))


def unpack_weight(words, scales):
    g, p, n, _ = words.shape
    vals = np.ascontiguousarray(words).view(ml_dtypes.float8_e4m3fn).astype(np.float64) * np.repeat(np.exp2(scales.astype(np.float64) - 127.0), 8, axis=1)[..., None]
    return vals.transpose(0, 1, 3, 2).reshape(g * 512, n)


def relu(v):
    return np.maximum(v, 0.0)


K, T, S, N, G, H = 512, 2048, 512, 512, 2048, 512
P = 2 ** 7


def setup_inputs():
    n = np.random.standard_normal
    s = mx_kscale(K)[:, None]
    u = mx_kscale(H)
    packed_xT = pack_weight(n((K, T)) * s)
    packed_dT = pack_weight(n((K, G)) / s)
    return {
        "x_words": packed_xT[0],
        "x_scales": packed_xT[1],
        "d_words": packed_dT[0],
        "d_scales": packed_dT[1],
        "cnt": np.tile(np.random.uniform(0.5, 1.5, S), (P, 1)).astype(np.float32),
        "gn": (np.random.uniform(0.5, 1.5, (H, 1)) * u[:, None]).astype(np.float32),
        "w1": (n((H, N)) / np.sqrt(H) / u[:, None]).astype(np.float32),
        "offs": striped(np.random.permutation(T)[:S]),
        "kidx": striped8(np.random.randint(0, G, (8, H))),
    }


def reference(x_words, x_scales, d_words, d_scales, cnt, gn, w1, offs, kidx):
    d_kidx = unpack_weight(d_words, d_scales)[np.arange(K)[:, None], runs(kidx, K)]
    xq = unpack_weight(x_words, x_scales)[:, unstriped(offs)]
    s = 0.0625 * (d_kidx.T @ xq)
    rp = relu(s)
    z = f64(gn) * ((rp) ** 2)
    return ((mxq(f64(w1), 0, "e4m3").T @ mxq(z, 0, "e4m3"))) * f64(cnt)[:1]

@@ -1,0 +1,212 @@
+from contextlib import ExitStack
+
+import concourse.mybir as mybir
+
+F32 = mybir.dt.float32
+BF16 = mybir.dt.bfloat16
+I32 = mybir.dt.int32
+U32 = mybir.dt.uint32
+U16 = mybir.dt.uint16
+U8 = mybir.dt.uint8
+FP8X4 = mybir.dt.float8_e4m3fn_x4
+ALU = mybir.AluOpType
+ACT = mybir.ActivationFunctionType
+
+K, T, S, N, G, H = 512, 2048, 512, 512, 2048, 512
+P = 128
+PACK = 4
+CH = 128
+FLOPS = 2 * K * H * S + 2 * H * N * S
+SCALAR_CHUNKS = (0,)
+
+
+def tile_picked_reluattn_relu_p_kernel(tc, x_words, x_scales, d_words, d_scales, cnt, gn, w1, offs, kidx, out):
+    nc = tc.nc
+    with ExitStack() as ctx:
+        keep = ctx.enter_context(tc.tile_pool(name="keep", bufs=1))
+        psum = ctx.enter_context(tc.psum_pool(name="psum", bufs=1))
+
+        kidx_t = keep.tile([P, H // 16], U16, name="kidx_t")
+        offs_t = keep.tile([P, S // 16], U16, name="offs_t")
+        ds_win = keep.tile([P, G], U8, name="ds_win", align_bytes=64)
+        xs_win = keep.tile([P, T], U8, name="xs_win", align_bytes=64)
+        d_win = keep.tile([P, G], I32, name="d_win", align_bytes=64)
+        x_win = keep.tile([P, T], I32, name="x_win", align_bytes=64)
+        w_raw = keep.tile([P, PACK, N], F32, name="w_raw", align_bytes=64)
+        gn_t = keep.tile([P, PACK], F32, name="gn_t")
+
+        nc.gpsimd.memset(ds_win[:].bitcast(I32), 0)
+        nc.vector.memset(xs_win[:].bitcast(I32), 0)
+        nc.sync.dma_start(kidx_t[:], kidx)
+        nc.sync.dma_start(offs_t[:], offs)
+        nc.scalar.dma_start(gn_t[:], gn.rearrange("(p t) o -> p (t o)", t=PACK))
+        nc.sync.dma_start(ds_win[0:P:8, :].bitcast(I32), d_scales[0].bitcast(I32))
+        nc.sync.dma_start(xs_win[0:P:8, :].bitcast(I32), x_scales[0].bitcast(I32))
+        nc.scalar.dma_start(w_raw[:], w1.rearrange("(p t) m -> p t m", t=PACK))
+        nc.scalar.dma_start(d_win[:], d_words[0].rearrange("p n t -> p (n t)").bitcast(I32))
+        nc.scalar.dma_start(x_win[:], x_words[0].rearrange("p n t -> p (n t)").bitcast(I32))
+
+        neg = keep.tile([P, PACK], F32, name="neg")
+        sign_b = keep.tile([P, PACK], BF16, name="sign_b")
+        mag = keep.tile([P, PACK], F32, name="mag")
+        root = keep.tile([P, PACK], F32, name="root")
+        nc.vector.tensor_scalar(neg[:], gn_t[:], 0.0, -2.0, ALU.is_lt, ALU.mult)
+        nc.vector.tensor_scalar(sign_b[:], neg[:], 1.0, None, ALU.add)
+        nc.scalar.activation(mag[:], gn_t[:], ACT.Abs)
+        nc.scalar.activation(root[:], mag[:], ACT.Sqrt, scale=0.0625 * 0.0625)
+
+        ds_got = keep.tile([P, H], U8, name="ds_got", align_bytes=64)
+        xs_got = keep.tile([P, S], U8, name="xs_got", align_bytes=64)
+        rows = keep.tile([P, H + S], U8, name="rows", align_bytes=64)
+        planes = keep.tile([P, H + S], U8, name="planes", align_bytes=64)
+        nc.gpsimd.memset(planes[:].bitcast(I32), 0)
+        nc.vector.tensor_copy(ds_got[:], ds_win[:].indirect(kidx_t[:]))
+        nc.vector.tensor_copy(xs_got[:], xs_win[:].indirect(offs_t[:]))
+        nc.vector.tensor_copy(
+            rows[:, 0:H].rearrange("p (t m) -> p m t", t=PACK),
+            ds_got[:].rearrange("p (m t) -> p m t", t=PACK),
+        )
+        nc.vector.tensor_copy(rows[:, H : H + S].bitcast(I32), xs_got[:].bitcast(I32))
+        for q in range(4):
+            nc.sync.dma_start(planes[32 * q : 32 * q + 4, :].bitcast(I32), rows[32 * q : 32 * q + 32 : 8, :].bitcast(I32))
+
+
+        halves = 2
+        hw = N // halves
+        w_codes = keep.tile([P, N], U32, name="w_codes", align_bytes=64)
+        w_scales = keep.tile([P, N], U8, name="w_scales", align_bytes=64)
+        w_cast = [keep.tile([P, hw, PACK], BF16, name="w_cast%d" % u, align_bytes=64) for u in range(halves)]
+        w_signed = [keep.tile([P, hw, PACK], BF16, name="w_signed%d" % u, align_bytes=64) for u in range(halves)]
+        for u in range(halves):
+            nc.scalar.copy(
+                w_cast[u][:].rearrange("p (c i) t -> p c t i", i=4),
+                w_raw[:, :, u * hw : (u + 1) * hw].rearrange("p t (c i) -> p c t i", i=4),
+            )
+
+        def sign_w(u):
+            nc.vector.tensor_tensor(
+                w_signed[u][:], w_cast[u][:], sign_b[:].unsqueeze(1).to_broadcast([P, hw, PACK]), ALU.mult
+            )
+
+        def quant_w(u):
+            cols = slice(u * hw, (u + 1) * hw)
+            nc.vector.quantize_mx(
+                out=w_codes[:, cols].bitcast(FP8X4),
+                scales=w_scales[:, cols],
+                in_=w_signed[u][:].rearrange("p m t -> p (m t)"),
+            )
+
+        d_got = keep.tile([P, H], U32, name="d_got", tag="late", align_bytes=64)
+        d_codes = keep.tile([P, H], U32, name="d_codes", align_bytes=64)
+        sign_w(0)
+        nc.vector.tensor_copy(d_got[:], d_win[:].bitcast(U32).indirect(kidx_t[:]))
+        quant_w(0)
+        nc.vector.tensor_copy(
+            d_codes[:].rearrange("p (t m) -> p m t", t=PACK),
+            d_got[:].rearrange("p (m t) -> p m t", t=PACK),
+        )
+        cnt_t = keep.tile([P, S], F32, name="cnt_t", tag="late", align_bytes=64)
+        nc.sync.dma_start(cnt_t[:], cnt)
+        sign_w(1)
+        quant_w(1)
+
+        gw = 256
+        x_got = [keep.tile([P, gw], U32, name="x_got%d" % u, align_bytes=64) for u in range(S // gw)]
+        for u in range(S // gw):
+            nc.vector.tensor_copy(
+                x_got[u][:], x_win[:].bitcast(U32).indirect(offs_t[:, u * gw // 16 : (u + 1) * gw // 16])
+            )
+
+        chunks = S // CH
+        scores = [psum.tile([P, PACK, CH], F32, name="scores%d" % c) for c in range(chunks)]
+        sums = [psum.tile([P, N // P, CH], F32, name="sums%d" % c) for c in range(chunks)]
+        pos = [keep.tile([P, CH * PACK], F32, name="pos%d" % c, align_bytes=64) for c in range(chunks)]
+        z = [keep.tile([P, CH * PACK], BF16, name="z%d" % c, align_bytes=64) for c in range(chunks)]
+        z_codes = [keep.tile([P, CH], U32, name="z_codes%d" % c, align_bytes=64) for c in range(chunks)]
+        z_scales = [keep.tile([P, CH], U8, name="z_scales%d" % c, align_bytes=64) for c in range(chunks)]
+        res = [keep.tile([P, N // P, CH], F32, name="res%d" % c, align_bytes=64) for c in range(chunks)]
+        out_v = out.rearrange("(a p) j -> p a j", p=P)
+
+        def score(c):
+            u, o = divmod(c * CH, gw)
+            for t in range(PACK):
+                nc.tensor.matmul_mx(
+                    out=scores[c][:, t, :],
+                    lhsT=d_codes[:, t * P : (t + 1) * P].bitcast(FP8X4),
+                    lhsT_scale=planes[:, t * P : (t + 1) * P],
+                    rhs=x_got[u][:, o : o + CH].bitcast(FP8X4),
+                    rhs_scale=planes[:, H + c * CH : H + (c + 1) * CH],
+                    start=True,
+                    stop=True,
+                )
+
+        def positive(c):
+            if c in SCALAR_CHUNKS:
+                for t in range(PACK):
+                    nc.scalar.activation(
+                        pos[c][:, t * CH : (t + 1) * CH], scores[c][:, t, :], ACT.Relu, scale=root[:, t : t + 1]
+                    )
+            else:
+                nc.vector.scalar_tensor_tensor(
+                    pos[c][:].rearrange("p (j t) -> p j t", t=PACK),
+                    scores[c][:].rearrange("p t j -> p j t"),
+                    0.0,
+                    root[:].unsqueeze(1).to_broadcast([P, CH, PACK]),
+                    ALU.max,
+                    ALU.mult,
+                )
+
+        def square(c):
+            if c in SCALAR_CHUNKS:
+                nc.scalar.activation(
+                    z[c][:].rearrange("p (c i t) -> p c t i", i=4, t=PACK),
+                    pos[c][:].rearrange("p (t c i) -> p c t i", i=4, t=PACK),
+                    ACT.Square,
+                )
+            else:
+                nc.scalar.activation(z[c][:], pos[c][:], ACT.Square)
+
+        def quant(c):
+            nc.vector.quantize_mx(out=z_codes[c][:].bitcast(FP8X4), scales=z_scales[c][:], in_=z[c][:])
+
+        def value(c):
+            for a in range(N // P):
+                nc.tensor.matmul_mx(
+                    out=sums[c][:, a, :],
+                    lhsT=w_codes[:, a * P : (a + 1) * P].bitcast(FP8X4),
+                    lhsT_scale=w_scales[:, a * P : (a + 1) * P],
+                    rhs=z_codes[c][:].bitcast(FP8X4),
+                    rhs_scale=z_scales[c][:],
+                    start=True,
+                    stop=True,
+                )
+
+        def finish(c):
+            cols = slice(c * CH, (c + 1) * CH)
+            nc.vector.tensor_tensor(
+                res[c][:], sums[c][:], cnt_t[:, cols].unsqueeze(1).to_broadcast([P, N // P, CH]), ALU.mult
+            )
+            nc.sync.dma_start(out_v[:, :, cols], res[c][:])
+
+        for c in range(chunks):
+            score(c)
+        positive(0)
+        positive(1)
+        square(0)
+        positive(2)
+        square(1)
+        quant(0)
+        value(0)
+        positive(3)
+        square(2)
+        quant(1)
+        value(1)
+        finish(0)
+        square(3)
+        quant(2)
+        value(2)
+        finish(1)
+        quant(3)
+        value(3)
+        finish(2)
+        finish(3)

@@ -31,27 +31,29 @@ def tile_picked_reluattn_relu_p_kernel(tc, x_words, x_scales, d_words, d_scales,
         ds_win = keep.tile([P, G], U8, name="ds_win", align_bytes=64)
         xs_win = keep.tile([P, T], U8, name="xs_win", align_bytes=64)
         d_win = keep.tile([P, G], I32, name="d_win", align_bytes=64)
-        x_win = keep.tile([P, T], I32, name="x_win", align_bytes=64)
-        w_raw = keep.tile([P, PACK, N], F32, name="w_raw", align_bytes=64)
+        x_win = keep.tile([P, T], I32, name="x_win", tag="x_then_w", align_bytes=64)
+        w_raw = [keep.tile([P, 2, N], F32, name="w_raw%d" % u, align_bytes=64) for u in range(2)]
         gn_t = keep.tile([P, PACK], F32, name="gn_t")
 
         nc.gpsimd.memset(ds_win[:].bitcast(I32), 0)
         nc.vector.memset(xs_win[:].bitcast(I32), 0)
+        w_rows = w1.rearrange("(p t) m -> p t m", t=PACK)
         nc.sync.dma_start(kidx_t[:], kidx)
-        nc.sync.dma_start(offs_t[:], offs)
         nc.scalar.dma_start(gn_t[:], gn.rearrange("(p t) o -> p (t o)", t=PACK))
+        nc.sync.dma_start(offs_t[:], offs)
+        nc.scalar.dma_start(w_raw[0][:], w_rows[:, 0:2, :])
         nc.sync.dma_start(ds_win[0:P:8, :].bitcast(I32), d_scales[0].bitcast(I32))
         nc.sync.dma_start(xs_win[0:P:8, :].bitcast(I32), x_scales[0].bitcast(I32))
-        nc.scalar.dma_start(w_raw[:], w1.rearrange("(p t) m -> p t m", t=PACK))
-        nc.scalar.dma_start(d_win[:], d_words[0].rearrange("p n t -> p (n t)").bitcast(I32))
-        nc.scalar.dma_start(x_win[:], x_words[0].rearrange("p n t -> p (n t)").bitcast(I32))
+        nc.sync.dma_start(w_raw[1][:], w_rows[:, 2:4, :])
+        nc.sync.dma_start(d_win[:], d_words[0].rearrange("p n t -> p (n t)").bitcast(I32))
+        nc.sync.dma_start(x_win[:], x_words[0].rearrange("p n t -> p (n t)").bitcast(I32))
 
         neg = keep.tile([P, PACK], F32, name="neg")
-        sign_b = keep.tile([P, PACK], BF16, name="sign_b")
+        sign = keep.tile([P, PACK], F32, name="sign")
         mag = keep.tile([P, PACK], F32, name="mag")
         root = keep.tile([P, PACK], F32, name="root")
         nc.vector.tensor_scalar(neg[:], gn_t[:], 0.0, -2.0, ALU.is_lt, ALU.mult)
-        nc.vector.tensor_scalar(sign_b[:], neg[:], 1.0, None, ALU.add)
+        nc.vector.tensor_scalar(sign[:], neg[:], 1.0, None, ALU.add)
         nc.scalar.activation(mag[:], gn_t[:], ACT.Abs)
         nc.scalar.activation(root[:], mag[:], ACT.Sqrt, scale=0.0625 * 0.0625)
 
@@ -73,19 +75,15 @@ def tile_picked_reluattn_relu_p_kernel(tc, x_words, x_scales, d_words, d_scales,
 
         halves = 2
         hw = N // halves
-        w_codes = keep.tile([P, N], U32, name="w_codes", align_bytes=64)
         w_scales = keep.tile([P, N], U8, name="w_scales", align_bytes=64)
-        w_cast = [keep.tile([P, hw, PACK], BF16, name="w_cast%d" % u, align_bytes=64) for u in range(halves)]
+        w_cast = keep.tile([P, PACK, N], BF16, name="w_cast", align_bytes=64)
         w_signed = [keep.tile([P, hw, PACK], BF16, name="w_signed%d" % u, align_bytes=64) for u in range(halves)]
+        for t in range(PACK):
+            nc.scalar.activation(w_cast[:, t, :], w_raw[t // 2][:, t % 2, :], ACT.Copy, scale=sign[:, t : t + 1])
         for u in range(halves):
             nc.scalar.copy(
-                w_cast[u][:].rearrange("p (c i) t -> p c t i", i=4),
-                w_raw[:, :, u * hw : (u + 1) * hw].rearrange("p t (c i) -> p c t i", i=4),
-            )
-
-        def sign_w(u):
-            nc.vector.tensor_tensor(
-                w_signed[u][:], w_cast[u][:], sign_b[:].unsqueeze(1).to_broadcast([P, hw, PACK]), ALU.mult
+                w_signed[u][:].rearrange("p (c i) t -> p c t i", i=4),
+                w_cast[:, :, u * hw : (u + 1) * hw].rearrange("p t (c i) -> p c t i", i=4),
             )
 
         def quant_w(u):
@@ -98,17 +96,13 @@ def tile_picked_reluattn_relu_p_kernel(tc, x_words, x_scales, d_words, d_scales,
 
         d_got = keep.tile([P, H], U32, name="d_got", tag="late", align_bytes=64)
         d_codes = keep.tile([P, H], U32, name="d_codes", align_bytes=64)
-        sign_w(0)
         nc.vector.tensor_copy(d_got[:], d_win[:].bitcast(U32).indirect(kidx_t[:]))
-        quant_w(0)
         nc.vector.tensor_copy(
             d_codes[:].rearrange("p (t m) -> p m t", t=PACK),
             d_got[:].rearrange("p (m t) -> p m t", t=PACK),
         )
         cnt_t = keep.tile([P, S], F32, name="cnt_t", tag="late", align_bytes=64)
         nc.sync.dma_start(cnt_t[:], cnt)
-        sign_w(1)
-        quant_w(1)
 
         gw = 256
         x_got = [keep.tile([P, gw], U32, name="x_got%d" % u, align_bytes=64) for u in range(S // gw)]
@@ -117,6 +111,9 @@ def tile_picked_reluattn_relu_p_kernel(tc, x_words, x_scales, d_words, d_scales,
                 x_got[u][:], x_win[:].bitcast(U32).indirect(offs_t[:, u * gw // 16 : (u + 1) * gw // 16])
             )
 
+        w_codes = keep.tile([P, N], U32, name="w_codes", tag="x_then_w", align_bytes=64)
+        quant_w(0)
+        quant_w(1)
         chunks = S // CH
         scores = [psum.tile([P, PACK, CH], F32, name="scores%d" % c) for c in range(chunks)]
         sums = [psum.tile([P, N // P, CH], F32, name="sums%d" % c) for c in range(chunks)]
@@ -201,12 +198,12 @@ def tile_picked_reluattn_relu_p_kernel(tc, x_words, x_scales, d_words, d_scales,
         square(2)
         quant(1)
         value(1)
-        finish(0)
         square(3)
         quant(2)
         value(2)
-        finish(1)
+        finish(0)
         quant(3)
         value(3)
+        finish(1)
         finish(2)
         finish(3)

@@ -17,7 +17,7 @@ P = 128
 PACK = 4
 CH = 128
 FLOPS = 2 * K * H * S + 2 * H * N * S
-SCALAR_CHUNKS = (0,)
+SCALAR_CHUNKS = (0, 3)
 
 
 def tile_picked_reluattn_relu_p_kernel(tc, x_words, x_scales, d_words, d_scales, cnt, gn, w1, offs, kidx, out):
@@ -39,12 +39,12 @@ def tile_picked_reluattn_relu_p_kernel(tc, x_words, x_scales, d_words, d_scales,
         nc.vector.memset(xs_win[:].bitcast(I32), 0)
         w_rows = w1.rearrange("(p t) m -> p t m", t=PACK)
         nc.sync.dma_start(kidx_t[:], kidx)
-        nc.scalar.dma_start(gn_t[:], gn.rearrange("(p t) o -> p (t o)", t=PACK))
-        nc.sync.dma_start(offs_t[:], offs)
         nc.scalar.dma_start(w_raw[0][:], w_rows[:, 0:2, :])
+        nc.sync.dma_start(gn_t[:], gn.rearrange("(p t) o -> p (t o)", t=PACK))
         nc.sync.dma_start(ds_win[0:P:8, :].bitcast(I32), d_scales[0].bitcast(I32))
-        nc.sync.dma_start(xs_win[0:P:8, :].bitcast(I32), x_scales[0].bitcast(I32))
         nc.sync.dma_start(w_raw[1][:], w_rows[:, 2:4, :])
+        nc.sync.dma_start(offs_t[:], offs)
+        nc.sync.dma_start(xs_win[0:P:8, :].bitcast(I32), x_scales[0].bitcast(I32))
         nc.sync.dma_start(d_win[:], d_words[0].rearrange("p n t -> p (n t)").bitcast(I32))
         nc.sync.dma_start(x_win[:], x_words[0].rearrange("p n t -> p (n t)").bitcast(I32))
 
@@ -63,11 +63,11 @@ def tile_picked_reluattn_relu_p_kernel(tc, x_words, x_scales, d_words, d_scales,
         planes = keep.tile([P, H + S], U8, name="planes", align_bytes=64)
         nc.gpsimd.memset(planes[:].bitcast(I32), 0)
         nc.vector.tensor_copy(ds_got[:], ds_win[:].indirect(kidx_t[:]))
-        nc.vector.tensor_copy(xs_got[:], xs_win[:].indirect(offs_t[:]))
         nc.vector.tensor_copy(
             rows[:, 0:H].rearrange("p (t m) -> p m t", t=PACK),
             ds_got[:].rearrange("p (m t) -> p m t", t=PACK),
         )
+        nc.vector.tensor_copy(xs_got[:], xs_win[:].indirect(offs_t[:]))
         nc.vector.tensor_copy(rows[:, H : H + S].bitcast(I32), xs_got[:].bitcast(I32))
         for q in range(4):
             nc.sync.dma_start(planes[32 * q : 32 * q + 4, :].bitcast(I32), rows[32 * q : 32 * q + 32 : 8, :].bitcast(I32))
@@ -118,10 +118,11 @@ def tile_picked_reluattn_relu_p_kernel(tc, x_words, x_scales, d_words, d_scales,
         scores = [psum.tile([P, PACK, CH], F32, name="scores%d" % c) for c in range(chunks)]
         sums = [psum.tile([P, N // P, CH], F32, name="sums%d" % c) for c in range(chunks)]
         pos = [keep.tile([P, CH * PACK], F32, name="pos%d" % c, align_bytes=64) for c in range(chunks)]
-        z = [keep.tile([P, CH * PACK], BF16, name="z%d" % c, align_bytes=64) for c in range(chunks)]
+        z = [keep.tile([P, CH * PACK], BF16, name="z%d" % c, align_bytes=64) for c in range(chunks - 1)]
+        z.append(keep.tile([P, CH * PACK], BF16, name="z_last", tag="z_then_res", align_bytes=64))
         z_codes = [keep.tile([P, CH], U32, name="z_codes%d" % c, align_bytes=64) for c in range(chunks)]
         z_scales = [keep.tile([P, CH], U8, name="z_scales%d" % c, align_bytes=64) for c in range(chunks)]
-        res = [keep.tile([P, N // P, CH], F32, name="res%d" % c, align_bytes=64) for c in range(chunks)]
+        res = {c: keep.tile([P, N // P, CH], F32, name="res%d" % c, align_bytes=64) for c in (0, 1, 3)}
         out_v = out.rearrange("(a p) j -> p a j", p=P)
 
         def score(c):
@@ -178,12 +179,15 @@ def tile_picked_reluattn_relu_p_kernel(tc, x_words, x_scales, d_words, d_scales,
                     stop=True,
                 )
 
-        def finish(c):
+        def finish(c, a0, a1, queue):
             cols = slice(c * CH, (c + 1) * CH)
             nc.vector.tensor_tensor(
-                res[c][:], sums[c][:], cnt_t[:, cols].unsqueeze(1).to_broadcast([P, N // P, CH]), ALU.mult
+                res[c][:, a0:a1, :],
+                sums[c][:, a0:a1, :],
+                cnt_t[:, cols].unsqueeze(1).to_broadcast([P, a1 - a0, CH]),
+                ALU.mult,
             )
-            nc.sync.dma_start(out_v[:, :, cols], res[c][:])
+            queue.dma_start(out_v[:, a0:a1, cols], res[c][:, a0:a1, :])
 
         for c in range(chunks):
             score(c)
@@ -194,16 +198,18 @@ def tile_picked_reluattn_relu_p_kernel(tc, x_words, x_scales, d_words, d_scales,
         square(1)
         quant(0)
         value(0)
-        positive(3)
         square(2)
         quant(1)
         value(1)
-        square(3)
+        positive(3)
+        finish(0, 0, 4, nc.sync)
         quant(2)
         value(2)
-        finish(0)
+        square(3)
+        finish(1, 0, 4, nc.sync)
         quant(3)
         value(3)
-        finish(1)
-        finish(2)
-        finish(3)
+        res[2] = keep.tile([P, N // P, CH], F32, name="res2", tag="z_then_res", align_bytes=64)
+        finish(2, 0, 4, nc.sync)
+        finish(3, 0, 2, nc.scalar)
+        finish(3, 2, 4, nc.sync)

@@ -18,6 +18,8 @@ PACK = 4
 CH = 128
 FLOPS = 2 * K * H * S + 2 * H * N * S
 SCALAR_CHUNKS = (0, 3)
+VECTOR_SLOTS = 1
+WARM = 8
 
 
 def tile_picked_reluattn_relu_p_kernel(tc, x_words, x_scales, d_words, d_scales, cnt, gn, w1, offs, kidx, out):
@@ -52,8 +54,8 @@ def tile_picked_reluattn_relu_p_kernel(tc, x_words, x_scales, d_words, d_scales,
         sign = keep.tile([P, PACK], F32, name="sign")
         mag = keep.tile([P, PACK], F32, name="mag")
         root = keep.tile([P, PACK], F32, name="root")
-        nc.vector.tensor_scalar(neg[:], gn_t[:], 0.0, -2.0, ALU.is_lt, ALU.mult)
-        nc.vector.tensor_scalar(sign[:], neg[:], 1.0, None, ALU.add)
+        nc.gpsimd.tensor_scalar(neg[:], gn_t[:], 0.0, -2.0, ALU.is_lt, ALU.mult)
+        nc.gpsimd.tensor_scalar(sign[:], neg[:], 1.0, 1.0, ALU.mult, ALU.add)
         nc.scalar.activation(mag[:], gn_t[:], ACT.Abs)
         nc.scalar.activation(root[:], mag[:], ACT.Sqrt, scale=0.0625 * 0.0625)
 
@@ -101,9 +103,9 @@ def tile_picked_reluattn_relu_p_kernel(tc, x_words, x_scales, d_words, d_scales,
             d_codes[:].rearrange("p (t m) -> p m t", t=PACK),
             d_got[:].rearrange("p (m t) -> p m t", t=PACK),
         )
+
         cnt_t = keep.tile([P, S], F32, name="cnt_t", tag="late", align_bytes=64)
         nc.sync.dma_start(cnt_t[:], cnt)
-
         gw = 256
         x_got = [keep.tile([P, gw], U32, name="x_got%d" % u, align_bytes=64) for u in range(S // gw)]
         for u in range(S // gw):
@@ -115,8 +117,13 @@ def tile_picked_reluattn_relu_p_kernel(tc, x_words, x_scales, d_words, d_scales,
         quant_w(0)
         quant_w(1)
         chunks = S // CH
-        scores = [psum.tile([P, PACK, CH], F32, name="scores%d" % c) for c in range(chunks)]
-        sums = [psum.tile([P, N // P, CH], F32, name="sums%d" % c) for c in range(chunks)]
+        first = [psum.tile([P, 2, CH], F32, name="first%d" % u, tag="first%d" % u) for u in range(2)]
+        scores = {c: psum.tile([P, PACK, CH], F32, name="scores%d" % c) for c in range(1, chunks)}
+        sums = {c: psum.tile([P, N // P, CH], F32, name="sums%d" % c) for c in range(chunks - 1)}
+
+        def slot(c, t):
+            return first[t // 2][:, t % 2, :] if c == 0 else scores[c][:, t, :]
+
         pos = [keep.tile([P, CH * PACK], F32, name="pos%d" % c, align_bytes=64) for c in range(chunks)]
         z = [keep.tile([P, CH * PACK], BF16, name="z%d" % c, align_bytes=64) for c in range(chunks - 1)]
         z.append(keep.tile([P, CH * PACK], BF16, name="z_last", tag="z_then_res", align_bytes=64))
@@ -129,7 +136,7 @@ def tile_picked_reluattn_relu_p_kernel(tc, x_words, x_scales, d_words, d_scales,
             u, o = divmod(c * CH, gw)
             for t in range(PACK):
                 nc.tensor.matmul_mx(
-                    out=scores[c][:, t, :],
+                    out=slot(c, t),
                     lhsT=d_codes[:, t * P : (t + 1) * P].bitcast(FP8X4),
                     lhsT_scale=planes[:, t * P : (t + 1) * P],
                     rhs=x_got[u][:, o : o + CH].bitcast(FP8X4),
@@ -141,9 +148,14 @@ def tile_picked_reluattn_relu_p_kernel(tc, x_words, x_scales, d_words, d_scales,
         def positive(c):
             if c in SCALAR_CHUNKS:
                 for t in range(PACK):
-                    nc.scalar.activation(
-                        pos[c][:, t * CH : (t + 1) * CH], scores[c][:, t, :], ACT.Relu, scale=root[:, t : t + 1]
-                    )
+                    if c == chunks - 1 and t < VECTOR_SLOTS:
+                        nc.vector.tensor_scalar(
+                            pos[c][:, t * CH : (t + 1) * CH], slot(c, t), 0.0, root[:, t : t + 1], ALU.max, ALU.mult
+                        )
+                    else:
+                        nc.scalar.activation(
+                            pos[c][:, t * CH : (t + 1) * CH], slot(c, t), ACT.Relu, scale=root[:, t : t + 1]
+                        )
             else:
                 nc.vector.scalar_tensor_tensor(
                     pos[c][:].rearrange("p (j t) -> p j t", t=PACK),
@@ -189,6 +201,16 @@ def tile_picked_reluattn_relu_p_kernel(tc, x_words, x_scales, d_words, d_scales,
             )
             queue.dma_start(out_v[:, a0:a1, cols], res[c][:, a0:a1, :])
 
+        for a in range(WARM):
+            nc.tensor.matmul_mx(
+                out=sums[a // 4][:, a % 4, :],
+                lhsT=d_codes[:, 0:P].bitcast(FP8X4),
+                lhsT_scale=rows[:, 0:P],
+                rhs=d_codes[:, 0:CH].bitcast(FP8X4),
+                rhs_scale=rows[:, 0:CH],
+                start=True,
+                stop=True,
+            )
         for c in range(chunks):
             score(c)
         positive(0)
@@ -199,15 +221,16 @@ def tile_picked_reluattn_relu_p_kernel(tc, x_words, x_scales, d_words, d_scales,
         quant(0)
         value(0)
         square(2)
+        positive(3)
         quant(1)
         value(1)
-        positive(3)
         finish(0, 0, 4, nc.sync)
         quant(2)
         value(2)
         square(3)
         finish(1, 0, 4, nc.sync)
         quant(3)
+        sums[3] = psum.tile([P, N // P, CH], F32, name="sums3", tag="first0")
         value(3)
         res[2] = keep.tile([P, N // P, CH], F32, name="res2", tag="z_then_res", align_bytes=64)
         finish(2, 0, 4, nc.sync)

@@ -17,9 +17,8 @@ P = 128
 PACK = 4
 CH = 128
 FLOPS = 2 * K * H * S + 2 * H * N * S
-SCALAR_CHUNKS = (0, 3)
-VECTOR_SLOTS = 1
-WARM = 8
+SCALAR_CHUNKS = (0,)
+VECTOR_SLOTS = 0
 
 
 def tile_picked_reluattn_relu_p_kernel(tc, x_words, x_scales, d_words, d_scales, cnt, gn, w1, offs, kidx, out):
@@ -32,9 +31,9 @@ def tile_picked_reluattn_relu_p_kernel(tc, x_words, x_scales, d_words, d_scales,
         offs_t = keep.tile([P, S // 16], U16, name="offs_t")
         ds_win = keep.tile([P, G], U8, name="ds_win", align_bytes=64)
         xs_win = keep.tile([P, T], U8, name="xs_win", align_bytes=64)
-        d_win = keep.tile([P, G], I32, name="d_win", align_bytes=64)
-        x_win = keep.tile([P, T], I32, name="x_win", tag="x_then_w", align_bytes=64)
-        w_raw = [keep.tile([P, 2, N], F32, name="w_raw%d" % u, align_bytes=64) for u in range(2)]
+        d_win = keep.tile([P, G], I32, name="d_win", tag="late", align_bytes=64)
+        x_win = keep.tile([P, T], I32, name="x_win", align_bytes=64)
+        w_raw = [keep.tile([P, 2, N], F32, name="w_raw%d" % u, tag="w_raw%d" % u, align_bytes=64) for u in range(2)]
         gn_t = keep.tile([P, PACK], F32, name="gn_t")
 
         nc.gpsimd.memset(ds_win[:].bitcast(I32), 0)
@@ -50,38 +49,34 @@ def tile_picked_reluattn_relu_p_kernel(tc, x_words, x_scales, d_words, d_scales,
         nc.sync.dma_start(d_win[:], d_words[0].rearrange("p n t -> p (n t)").bitcast(I32))
         nc.sync.dma_start(x_win[:], x_words[0].rearrange("p n t -> p (n t)").bitcast(I32))
 
-        neg = keep.tile([P, PACK], F32, name="neg")
         sign = keep.tile([P, PACK], F32, name="sign")
         mag = keep.tile([P, PACK], F32, name="mag")
         root = keep.tile([P, PACK], F32, name="root")
-        nc.gpsimd.tensor_scalar(neg[:], gn_t[:], 0.0, -2.0, ALU.is_lt, ALU.mult)
-        nc.gpsimd.tensor_scalar(sign[:], neg[:], 1.0, 1.0, ALU.mult, ALU.add)
-        nc.scalar.activation(mag[:], gn_t[:], ACT.Abs)
-        nc.scalar.activation(root[:], mag[:], ACT.Sqrt, scale=0.0625 * 0.0625)
-
-        ds_got = keep.tile([P, H], U8, name="ds_got", align_bytes=64)
-        xs_got = keep.tile([P, S], U8, name="xs_got", align_bytes=64)
-        rows = keep.tile([P, H + S], U8, name="rows", align_bytes=64)
-        planes = keep.tile([P, H + S], U8, name="planes", align_bytes=64)
-        nc.gpsimd.memset(planes[:].bitcast(I32), 0)
-        nc.vector.tensor_copy(ds_got[:], ds_win[:].indirect(kidx_t[:]))
-        nc.vector.tensor_copy(
-            rows[:, 0:H].rearrange("p (t m) -> p m t", t=PACK),
-            ds_got[:].rearrange("p (m t) -> p m t", t=PACK),
-        )
-        nc.vector.tensor_copy(xs_got[:], xs_win[:].indirect(offs_t[:]))
-        nc.vector.tensor_copy(rows[:, H : H + S].bitcast(I32), xs_got[:].bitcast(I32))
-        for q in range(4):
-            nc.sync.dma_start(planes[32 * q : 32 * q + 4, :].bitcast(I32), rows[32 * q : 32 * q + 32 : 8, :].bitcast(I32))
-
+        nc.vector.scalar_tensor_tensor(mag[:], gn_t[:], -1.0, gn_t[:], ALU.mult, ALU.max)
+        nc.vector.tensor_scalar(sign[:], gn_t[:], 0.0, 0.5, ALU.is_ge, ALU.subtract)
+        nc.scalar.activation(root[:], mag[:], ACT.Sqrt, scale=2.0 * 0.0625 * 0.0625)
 
         halves = 2
         hw = N // halves
         w_scales = keep.tile([P, N], U8, name="w_scales", align_bytes=64)
         w_cast = keep.tile([P, PACK, N], BF16, name="w_cast", align_bytes=64)
-        w_signed = [keep.tile([P, hw, PACK], BF16, name="w_signed%d" % u, align_bytes=64) for u in range(halves)]
+        w_signed = [keep.tile([P, hw, PACK], BF16, name="w_signed%d" % u, tag="w_signed%d" % u, align_bytes=64) for u in range(halves)]
         for t in range(PACK):
             nc.scalar.activation(w_cast[:, t, :], w_raw[t // 2][:, t % 2, :], ACT.Copy, scale=sign[:, t : t + 1])
+
+        ds_got = keep.tile([P, H], U8, name="ds_got", align_bytes=64)
+        xs_got = keep.tile([P, S], U8, name="xs_got", align_bytes=64)
+        planes = keep.tile([P, H + S], U8, name="planes", align_bytes=64)
+        nc.vector.tensor_copy(ds_got[:], ds_win[:].indirect(kidx_t[:]))
+        nc.vector.tensor_copy(xs_got[:], xs_win[:].indirect(offs_t[:]))
+        nc.vector.tensor_copy(
+            planes[:, 0:H].rearrange("p (t m) -> p m t", t=PACK),
+            ds_got[:].rearrange("p (m t) -> p m t", t=PACK),
+        )
+        nc.vector.tensor_copy(planes[:, H : H + S].bitcast(I32), xs_got[:].bitcast(I32))
+        for r in range(1, 4):
+            nc.sync.dma_start(planes[r:P:32, :].bitcast(I32), planes[8 * r : P : 32, :].bitcast(I32))
+
         for u in range(halves):
             nc.scalar.copy(
                 w_signed[u][:].rearrange("p (c i) t -> p c t i", i=4),
@@ -96,26 +91,27 @@ def tile_picked_reluattn_relu_p_kernel(tc, x_words, x_scales, d_words, d_scales,
                 in_=w_signed[u][:].rearrange("p m t -> p (m t)"),
             )
 
-        d_got = keep.tile([P, H], U32, name="d_got", tag="late", align_bytes=64)
         d_codes = keep.tile([P, H], U32, name="d_codes", align_bytes=64)
+        d_got = keep.tile([P, H], U32, name="d_got", align_bytes=64)
         nc.vector.tensor_copy(d_got[:], d_win[:].bitcast(U32).indirect(kidx_t[:]))
         nc.vector.tensor_copy(
             d_codes[:].rearrange("p (t m) -> p m t", t=PACK),
             d_got[:].rearrange("p (m t) -> p m t", t=PACK),
         )
 
+        w_codes = keep.tile([P, N], U32, name="w_codes", align_bytes=64)
+        quant_w(0)
+        quant_w(1)
         cnt_t = keep.tile([P, S], F32, name="cnt_t", tag="late", align_bytes=64)
         nc.sync.dma_start(cnt_t[:], cnt)
         gw = 256
-        x_got = [keep.tile([P, gw], U32, name="x_got%d" % u, align_bytes=64) for u in range(S // gw)]
+        x_all = keep.tile([P, S], U32, name="x_all", tag="w_signed1", align_bytes=64)
+        x_got = [x_all[:, u * gw : (u + 1) * gw] for u in range(S // gw)]
         for u in range(S // gw):
             nc.vector.tensor_copy(
-                x_got[u][:], x_win[:].bitcast(U32).indirect(offs_t[:, u * gw // 16 : (u + 1) * gw // 16])
+                x_got[u], x_win[:].bitcast(U32).indirect(offs_t[:, u * gw // 16 : (u + 1) * gw // 16])
             )
 
-        w_codes = keep.tile([P, N], U32, name="w_codes", tag="x_then_w", align_bytes=64)
-        quant_w(0)
-        quant_w(1)
         chunks = S // CH
         first = [psum.tile([P, 2, CH], F32, name="first%d" % u, tag="first%d" % u) for u in range(2)]
         scores = {c: psum.tile([P, PACK, CH], F32, name="scores%d" % c) for c in range(1, chunks)}
@@ -124,12 +120,12 @@ def tile_picked_reluattn_relu_p_kernel(tc, x_words, x_scales, d_words, d_scales,
         def slot(c, t):
             return first[t // 2][:, t % 2, :] if c == 0 else scores[c][:, t, :]
 
-        pos = [keep.tile([P, CH * PACK], F32, name="pos%d" % c, align_bytes=64) for c in range(chunks)]
+        pos = [keep.tile([P, CH * PACK], F32, name="pos%d" % c, tag="pos%d" % c, align_bytes=64) for c in range(chunks - 1)]
         z = [keep.tile([P, CH * PACK], BF16, name="z%d" % c, align_bytes=64) for c in range(chunks - 1)]
         z.append(keep.tile([P, CH * PACK], BF16, name="z_last", tag="z_then_res", align_bytes=64))
         z_codes = [keep.tile([P, CH], U32, name="z_codes%d" % c, align_bytes=64) for c in range(chunks)]
         z_scales = [keep.tile([P, CH], U8, name="z_scales%d" % c, align_bytes=64) for c in range(chunks)]
-        res = {c: keep.tile([P, N // P, CH], F32, name="res%d" % c, align_bytes=64) for c in (0, 1, 3)}
+        res = {c: keep.tile([P, N // P, CH], F32, name="res%d" % c, align_bytes=64) for c in range(chunks)}
         out_v = out.rearrange("(a p) j -> p a j", p=P)
 
         def score(c):
@@ -182,7 +178,7 @@ def tile_picked_reluattn_relu_p_kernel(tc, x_words, x_scales, d_words, d_scales,
         def value(c):
             for a in range(N // P):
                 nc.tensor.matmul_mx(
-                    out=sums[c][:, a, :],
+                    out=sums[c][:, a, :] if c < chunks - 1 else last[a // 2][:, a % 2, :],
                     lhsT=w_codes[:, a * P : (a + 1) * P].bitcast(FP8X4),
                     lhsT_scale=w_scales[:, a * P : (a + 1) * P],
                     rhs=z_codes[c][:].bitcast(FP8X4),
@@ -195,19 +191,19 @@ def tile_picked_reluattn_relu_p_kernel(tc, x_words, x_scales, d_words, d_scales,
             cols = slice(c * CH, (c + 1) * CH)
             nc.vector.tensor_tensor(
                 res[c][:, a0:a1, :],
-                sums[c][:, a0:a1, :],
+                sums[c][:, a0:a1, :] if c < chunks - 1 else last[a0 // 2][:],
                 cnt_t[:, cols].unsqueeze(1).to_broadcast([P, a1 - a0, CH]),
                 ALU.mult,
             )
             queue.dma_start(out_v[:, a0:a1, cols], res[c][:, a0:a1, :])
 
-        for a in range(WARM):
+        for a in range(2):
             nc.tensor.matmul_mx(
-                out=sums[a // 4][:, a % 4, :],
+                out=sums[a][:].rearrange("p a j -> p (a j)"),
                 lhsT=d_codes[:, 0:P].bitcast(FP8X4),
-                lhsT_scale=rows[:, 0:P],
-                rhs=d_codes[:, 0:CH].bitcast(FP8X4),
-                rhs_scale=rows[:, 0:CH],
+                lhsT_scale=ds_got[:, 0:P],
+                rhs=d_codes[:].bitcast(FP8X4),
+                rhs_scale=ds_got[:],
                 start=True,
                 stop=True,
             )
@@ -220,19 +216,19 @@ def tile_picked_reluattn_relu_p_kernel(tc, x_words, x_scales, d_words, d_scales,
         square(1)
         quant(0)
         value(0)
-        square(2)
+        pos.append(keep.tile([P, CH * PACK], F32, name="pos3", tag="pos0", align_bytes=64))
         positive(3)
+        square(2)
         quant(1)
         value(1)
+        square(3)
         finish(0, 0, 4, nc.sync)
         quant(2)
         value(2)
-        square(3)
         finish(1, 0, 4, nc.sync)
         quant(3)
-        sums[3] = psum.tile([P, N // P, CH], F32, name="sums3", tag="first0")
+        last = [psum.tile([P, 2, CH], F32, name="last%d" % u, tag="first%d" % u) for u in range(2)]
         value(3)
-        res[2] = keep.tile([P, N // P, CH], F32, name="res2", tag="z_then_res", align_bytes=64)
         finish(2, 0, 4, nc.sync)
         finish(3, 0, 2, nc.scalar)
         finish(3, 2, 4, nc.sync)

@@ -32,11 +32,11 @@ def tile_picked_reluattn_relu_p_kernel(tc, x_words, x_scales, d_words, d_scales,
         ds_win = keep.tile([P, G], U8, name="ds_win", align_bytes=64)
         xs_win = keep.tile([P, T], U8, name="xs_win", align_bytes=64)
         d_win = keep.tile([P, G], I32, name="d_win", tag="late", align_bytes=64)
-        x_win = keep.tile([P, T], I32, name="x_win", align_bytes=64)
+        x_win = keep.tile([P, T], I32, name="x_win", tag="x_then_w", align_bytes=64)
         w_raw = [keep.tile([P, 2, N], F32, name="w_raw%d" % u, tag="w_raw%d" % u, align_bytes=64) for u in range(2)]
         gn_t = keep.tile([P, PACK], F32, name="gn_t")
 
-        nc.gpsimd.memset(ds_win[:].bitcast(I32), 0)
+        nc.vector.memset(ds_win[:].bitcast(I32), 0)
         nc.vector.memset(xs_win[:].bitcast(I32), 0)
         w_rows = w1.rearrange("(p t) m -> p t m", t=PACK)
         nc.sync.dma_start(kidx_t[:], kidx)
@@ -86,7 +86,7 @@ def tile_picked_reluattn_relu_p_kernel(tc, x_words, x_scales, d_words, d_scales,
         def quant_w(u):
             cols = slice(u * hw, (u + 1) * hw)
             nc.vector.quantize_mx(
-                out=w_codes[:, cols].bitcast(FP8X4),
+                out=w_codes[u][:].bitcast(FP8X4),
                 scales=w_scales[:, cols],
                 in_=w_signed[u][:].rearrange("p m t -> p (m t)"),
             )
@@ -99,19 +99,20 @@ def tile_picked_reluattn_relu_p_kernel(tc, x_words, x_scales, d_words, d_scales,
             d_got[:].rearrange("p (m t) -> p m t", t=PACK),
         )
 
-        w_codes = keep.tile([P, N], U32, name="w_codes", align_bytes=64)
+        w_codes = [keep.tile([P, hw], U32, name="w_codes0", align_bytes=64)]
         quant_w(0)
-        quant_w(1)
         cnt_t = keep.tile([P, S], F32, name="cnt_t", tag="late", align_bytes=64)
         nc.sync.dma_start(cnt_t[:], cnt)
         gw = 256
-        x_all = keep.tile([P, S], U32, name="x_all", tag="w_signed1", align_bytes=64)
+        x_all = keep.tile([P, S], U32, name="x_all", tag="w_signed0", align_bytes=64)
         x_got = [x_all[:, u * gw : (u + 1) * gw] for u in range(S // gw)]
         for u in range(S // gw):
             nc.vector.tensor_copy(
                 x_got[u], x_win[:].bitcast(U32).indirect(offs_t[:, u * gw // 16 : (u + 1) * gw // 16])
             )
 
+        w_codes.append(keep.tile([P, hw], U32, name="w_codes1", tag="x_then_w", align_bytes=64))
+        quant_w(1)
         chunks = S // CH
         first = [psum.tile([P, 2, CH], F32, name="first%d" % u, tag="first%d" % u) for u in range(2)]
         scores = {c: psum.tile([P, PACK, CH], F32, name="scores%d" % c) for c in range(1, chunks)}
@@ -179,7 +180,7 @@ def tile_picked_reluattn_relu_p_kernel(tc, x_words, x_scales, d_words, d_scales,
             for a in range(N // P):
                 nc.tensor.matmul_mx(
                     out=sums[c][:, a, :] if c < chunks - 1 else last[a // 2][:, a % 2, :],
-                    lhsT=w_codes[:, a * P : (a + 1) * P].bitcast(FP8X4),
+                    lhsT=w_codes[a // 2][:, a % 2 * P : (a % 2 + 1) * P].bitcast(FP8X4),
                     lhsT_scale=w_scales[:, a * P : (a + 1) * P],
                     rhs=z_codes[c][:].bitcast(FP8X4),
                     rhs_scale=z_scales[c][:],
@@ -200,9 +201,9 @@ def tile_picked_reluattn_relu_p_kernel(tc, x_words, x_scales, d_words, d_scales,
         for a in range(2):
             nc.tensor.matmul_mx(
                 out=sums[a][:].rearrange("p a j -> p (a j)"),
-                lhsT=d_codes[:, 0:P].bitcast(FP8X4),
+                lhsT=d_got[:, 0:P].bitcast(FP8X4),
                 lhsT_scale=ds_got[:, 0:P],
-                rhs=d_codes[:].bitcast(FP8X4),
+                rhs=d_got[:].bitcast(FP8X4),
                 rhs_scale=ds_got[:],
                 start=True,
                 stop=True,

@@ -122,7 +122,7 @@ def tile_picked_reluattn_relu_p_kernel(tc, x_words, x_scales, d_words, d_scales,
             return first[t // 2][:, t % 2, :] if c == 0 else scores[c][:, t, :]
 
         pos = [keep.tile([P, CH * PACK], F32, name="pos%d" % c, tag="pos%d" % c, align_bytes=64) for c in range(chunks - 1)]
-        z = [keep.tile([P, CH * PACK], BF16, name="z%d" % c, align_bytes=64) for c in range(chunks - 1)]
+        z = [keep.tile([P, CH * PACK], BF16, name="z%d" % c, tag="z%d" % c, align_bytes=64) for c in range(chunks - 1)]
         z.append(keep.tile([P, CH * PACK], BF16, name="z_last", tag="z_then_res", align_bytes=64))
         z_codes = [keep.tile([P, CH], U32, name="z_codes%d" % c, align_bytes=64) for c in range(chunks)]
         z_scales = [keep.tile([P, CH], U8, name="z_scales%d" % c, align_bytes=64) for c in range(chunks)]
@@ -218,11 +218,27 @@ def tile_picked_reluattn_relu_p_kernel(tc, x_words, x_scales, d_words, d_scales,
         quant(0)
         value(0)
         pos.append(keep.tile([P, CH * PACK], F32, name="pos3", tag="pos0", align_bytes=64))
-        positive(3)
+        hq = CH // 2
+        nc.vector.scalar_tensor_tensor(
+            pos[3][:, 0 : hq * PACK].rearrange("p (j t) -> p j t", t=PACK),
+            scores[3][:, :, 0:hq].rearrange("p t j -> p j t"),
+            0.0,
+            root[:].unsqueeze(1).to_broadcast([P, hq, PACK]),
+            ALU.max,
+            ALU.mult,
+        )
+        pos_s = keep.tile([P, PACK, hq], F32, name="pos_s", tag="z0", align_bytes=64)
+        for t in range(PACK):
+            nc.scalar.activation(pos_s[:, t, :], scores[3][:, t, hq:CH], ACT.Relu, scale=root[:, t : t + 1])
         square(2)
         quant(1)
         value(1)
-        square(3)
+        nc.scalar.activation(
+            z[3][:, hq * PACK :].rearrange("p (c i t) -> p c t i", i=4, t=PACK),
+            pos_s[:].rearrange("p t (c i) -> p c t i", i=4),
+            ACT.Square,
+        )
+        nc.scalar.activation(z[3][:, 0 : hq * PACK], pos[3][:, 0 : hq * PACK], ACT.Square)
         finish(0, 0, 4, nc.sync)
         quant(2)
         value(2)
@@ -230,6 +246,6 @@ def tile_picked_reluattn_relu_p_kernel(tc, x_words, x_scales, d_words, d_scales,
         quant(3)
         last = [psum.tile([P, 2, CH], F32, name="last%d" % u, tag="first%d" % u) for u in range(2)]
         value(3)
-        finish(2, 0, 4, nc.sync)
-        finish(3, 0, 2, nc.scalar)
-        finish(3, 2, 4, nc.sync)
+        finish(2, 0, 4, nc.scalar)
+        finish(3, 0, 2, nc.sync)
+        finish(3, 2, 4, nc.scalar)

@@ -66,7 +66,7 @@ def tile_picked_reluattn_relu_p_kernel(tc, x_words, x_scales, d_words, d_scales,
 
         ds_got = keep.tile([P, H], U8, name="ds_got", align_bytes=64)
         xs_got = keep.tile([P, S], U8, name="xs_got", align_bytes=64)
-        planes = keep.tile([P, H + S], U8, name="planes", align_bytes=64)
+        planes = keep.tile([P, H + S], U8, name="planes", tag="w_raw1", align_bytes=64)
         nc.vector.tensor_copy(ds_got[:], ds_win[:].indirect(kidx_t[:]))
         nc.vector.tensor_copy(xs_got[:], xs_win[:].indirect(offs_t[:]))
         nc.vector.tensor_copy(
@@ -75,7 +75,7 @@ def tile_picked_reluattn_relu_p_kernel(tc, x_words, x_scales, d_words, d_scales,
         )
         nc.vector.tensor_copy(planes[:, H : H + S].bitcast(I32), xs_got[:].bitcast(I32))
         for r in range(1, 4):
-            nc.sync.dma_start(planes[r:P:32, :].bitcast(I32), planes[8 * r : P : 32, :].bitcast(I32))
+            nc.scalar.dma_start(planes[r:P:32, :].bitcast(I32), planes[8 * r : P : 32, :].bitcast(I32))
 
         for u in range(halves):
             nc.scalar.copy(
@@ -86,7 +86,7 @@ def tile_picked_reluattn_relu_p_kernel(tc, x_words, x_scales, d_words, d_scales,
         def quant_w(u):
             cols = slice(u * hw, (u + 1) * hw)
             nc.vector.quantize_mx(
-                out=w_codes[u][:].bitcast(FP8X4),
+                out=w_codes[u].bitcast(FP8X4),
                 scales=w_scales[:, cols],
                 in_=w_signed[u][:].rearrange("p m t -> p (m t)"),
             )
@@ -99,19 +99,19 @@ def tile_picked_reluattn_relu_p_kernel(tc, x_words, x_scales, d_words, d_scales,
             d_got[:].rearrange("p (m t) -> p m t", t=PACK),
         )
 
-        w_codes = [keep.tile([P, hw], U32, name="w_codes0", align_bytes=64)]
-        quant_w(0)
         cnt_t = keep.tile([P, S], F32, name="cnt_t", tag="late", align_bytes=64)
         nc.sync.dma_start(cnt_t[:], cnt)
         gw = 256
-        x_all = keep.tile([P, S], U32, name="x_all", tag="w_signed0", align_bytes=64)
+        x_all = keep.tile([P, S], U32, name="x_all", align_bytes=64)
         x_got = [x_all[:, u * gw : (u + 1) * gw] for u in range(S // gw)]
         for u in range(S // gw):
             nc.vector.tensor_copy(
                 x_got[u], x_win[:].bitcast(U32).indirect(offs_t[:, u * gw // 16 : (u + 1) * gw // 16])
             )
 
-        w_codes.append(keep.tile([P, hw], U32, name="w_codes1", tag="x_then_w", align_bytes=64))
+        both = keep.tile([P, N], U32, name="w_codes", tag="x_then_w", align_bytes=64)
+        w_codes = [both[:, u * hw : (u + 1) * hw] for u in range(halves)]
+        quant_w(0)
         quant_w(1)
         chunks = S // CH
         first = [psum.tile([P, 2, CH], F32, name="first%d" % u, tag="first%d" % u) for u in range(2)]

@@ -17,8 +17,6 @@ P = 128
 PACK = 4
 CH = 128
 FLOPS = 2 * K * H * S + 2 * H * N * S
-SCALAR_CHUNKS = (0,)
-VECTOR_SLOTS = 0
 
 
 def tile_picked_reluattn_relu_p_kernel(tc, x_words, x_scales, d_words, d_scales, cnt, gn, w1, offs, kidx, out):
@@ -31,23 +29,27 @@ def tile_picked_reluattn_relu_p_kernel(tc, x_words, x_scales, d_words, d_scales,
         offs_t = keep.tile([P, S // 16], U16, name="offs_t")
         ds_win = keep.tile([P, G], U8, name="ds_win", align_bytes=64)
         xs_win = keep.tile([P, T], U8, name="xs_win", align_bytes=64)
-        d_win = keep.tile([P, G], I32, name="d_win", tag="late", align_bytes=64)
-        x_win = keep.tile([P, T], I32, name="x_win", tag="x_then_w", align_bytes=64)
-        w_raw = [keep.tile([P, 2, N], F32, name="w_raw%d" % u, tag="w_raw%d" % u, align_bytes=64) for u in range(2)]
+        d_win = keep.tile([P, G], I32, name="d_win", tag="d_then_cnt", align_bytes=64)
+        x_win = keep.tile([P, T], I32, name="x_win", tag="x_then_woven", align_bytes=64)
         gn_t = keep.tile([P, PACK], F32, name="gn_t")
+        hw = N // 2
+        w_raw = [keep.tile([P, 2, hw], F32, name="w_raw%d" % u, align_bytes=64) for u in range(2)]
 
-        nc.vector.memset(ds_win[:].bitcast(I32), 0)
-        nc.vector.memset(xs_win[:].bitcast(I32), 0)
+        for win in (ds_win, xs_win):
+            nc.vector.memset(win[:, 0:1024].bitcast(I32), 0)
+            nc.gpsimd.memset(win[:, 1024:2048].bitcast(I32), 0)
         w_rows = w1.rearrange("(p t) m -> p t m", t=PACK)
+        nc.scalar.dma_start(gn_t[:], gn.rearrange("(p t) o -> p (t o)", t=PACK))
+        nc.scalar.dma_start(w_raw[0][:], w_rows[:, 0:2, 0:hw])
         nc.sync.dma_start(kidx_t[:], kidx)
-        nc.scalar.dma_start(w_raw[0][:], w_rows[:, 0:2, :])
-        nc.sync.dma_start(gn_t[:], gn.rearrange("(p t) o -> p (t o)", t=PACK))
-        nc.sync.dma_start(ds_win[0:P:8, :].bitcast(I32), d_scales[0].bitcast(I32))
-        nc.sync.dma_start(w_raw[1][:], w_rows[:, 2:4, :])
         nc.sync.dma_start(offs_t[:], offs)
+        nc.sync.dma_start(ds_win[0:P:8, :].bitcast(I32), d_scales[0].bitcast(I32))
         nc.sync.dma_start(xs_win[0:P:8, :].bitcast(I32), x_scales[0].bitcast(I32))
+        nc.sync.dma_start(w_raw[1][:], w_rows[:, 2:4, 0:hw])
         nc.sync.dma_start(d_win[:], d_words[0].rearrange("p n t -> p (n t)").bitcast(I32))
         nc.sync.dma_start(x_win[:], x_words[0].rearrange("p n t -> p (n t)").bitcast(I32))
+        w_late = [keep.tile([P, 2, hw], F32, name="w_late0", align_bytes=64)]
+        nc.sync.dma_start(w_late[0][:], w_rows[:, 0:2, hw:N])
 
         sign = keep.tile([P, PACK], F32, name="sign")
         mag = keep.tile([P, PACK], F32, name="mag")
@@ -56,17 +58,19 @@ def tile_picked_reluattn_relu_p_kernel(tc, x_words, x_scales, d_words, d_scales,
         nc.vector.tensor_scalar(sign[:], gn_t[:], 0.0, 0.5, ALU.is_ge, ALU.subtract)
         nc.scalar.activation(root[:], mag[:], ACT.Sqrt, scale=2.0 * 0.0625 * 0.0625)
 
-        halves = 2
-        hw = N // halves
         w_scales = keep.tile([P, N], U8, name="w_scales", align_bytes=64)
-        w_cast = keep.tile([P, PACK, N], BF16, name="w_cast", align_bytes=64)
-        w_signed = [keep.tile([P, hw, PACK], BF16, name="w_signed%d" % u, tag="w_signed%d" % u, align_bytes=64) for u in range(halves)]
+        cast_early = keep.tile([P, PACK, hw], BF16, name="cast_early", align_bytes=64)
+        woven_early = keep.tile([P, hw, PACK], BF16, name="woven_early", align_bytes=64)
         for t in range(PACK):
-            nc.scalar.activation(w_cast[:, t, :], w_raw[t // 2][:, t % 2, :], ACT.Copy, scale=sign[:, t : t + 1])
+            nc.scalar.activation(cast_early[:, t, :], w_raw[t // 2][:, t % 2, :], ACT.Copy, scale=sign[:, t : t + 1])
+        nc.scalar.copy(
+            woven_early[:].rearrange("p (c i) t -> p c t i", i=4),
+            cast_early[:].rearrange("p t (c i) -> p c t i", i=4),
+        )
 
         ds_got = keep.tile([P, H], U8, name="ds_got", align_bytes=64)
-        xs_got = keep.tile([P, S], U8, name="xs_got", align_bytes=64)
-        planes = keep.tile([P, H + S], U8, name="planes", tag="w_raw1", align_bytes=64)
+        xs_got = keep.tile([P, S], U8, name="xs_got", tag="xs_then_w", align_bytes=64)
+        planes = keep.tile([P, H + S], U8, name="planes", align_bytes=64)
         nc.vector.tensor_copy(ds_got[:], ds_win[:].indirect(kidx_t[:]))
         nc.vector.tensor_copy(xs_got[:], xs_win[:].indirect(offs_t[:]))
         nc.vector.tensor_copy(
@@ -75,96 +79,85 @@ def tile_picked_reluattn_relu_p_kernel(tc, x_words, x_scales, d_words, d_scales,
         )
         nc.vector.tensor_copy(planes[:, H : H + S].bitcast(I32), xs_got[:].bitcast(I32))
         for r in range(1, 4):
-            nc.scalar.dma_start(planes[r:P:32, :].bitcast(I32), planes[8 * r : P : 32, :].bitcast(I32))
+            nc.sync.dma_start(planes[r:P:32, :].bitcast(I32), planes[8 * r : P : 32, :].bitcast(I32))
+        w_late.append(keep.tile([P, 2, hw], F32, name="w_late1", tag="xs_then_w", align_bytes=64))
+        nc.sync.dma_start(w_late[1][:], w_rows[:, 2:4, hw:N])
+        cast_late = keep.tile([P, PACK, hw], BF16, name="cast_late", align_bytes=64)
+        for t in range(PACK):
+            nc.gpsimd.tensor_scalar(cast_late[:, t, :], w_late[t // 2][:, t % 2, :], sign[:, t : t + 1], 0.0, ALU.mult, ALU.add)
 
-        for u in range(halves):
-            nc.scalar.copy(
-                w_signed[u][:].rearrange("p (c i) t -> p c t i", i=4),
-                w_cast[:, :, u * hw : (u + 1) * hw].rearrange("p t (c i) -> p c t i", i=4),
-            )
-
-        def quant_w(u):
-            cols = slice(u * hw, (u + 1) * hw)
+        def quant_w(woven, c0, c1):
             nc.vector.quantize_mx(
-                out=w_codes[u].bitcast(FP8X4),
-                scales=w_scales[:, cols],
-                in_=w_signed[u][:].rearrange("p m t -> p (m t)"),
+                out=w_codes[:, c0:c1].bitcast(FP8X4),
+                scales=w_scales[:, c0:c1],
+                in_=woven.rearrange("p m t -> p (m t)"),
             )
 
         d_codes = keep.tile([P, H], U32, name="d_codes", align_bytes=64)
-        d_got = keep.tile([P, H], U32, name="d_got", align_bytes=64)
+        d_got = keep.tile([P, H], U32, name="d_got", tag="got_then_cnt", align_bytes=64)
         nc.vector.tensor_copy(d_got[:], d_win[:].bitcast(U32).indirect(kidx_t[:]))
         nc.vector.tensor_copy(
             d_codes[:].rearrange("p (t m) -> p m t", t=PACK),
             d_got[:].rearrange("p (m t) -> p m t", t=PACK),
         )
 
-        cnt_t = keep.tile([P, S], F32, name="cnt_t", tag="late", align_bytes=64)
-        nc.sync.dma_start(cnt_t[:], cnt)
         gw = 256
         x_all = keep.tile([P, S], U32, name="x_all", align_bytes=64)
-        x_got = [x_all[:, u * gw : (u + 1) * gw] for u in range(S // gw)]
         for u in range(S // gw):
             nc.vector.tensor_copy(
-                x_got[u], x_win[:].bitcast(U32).indirect(offs_t[:, u * gw // 16 : (u + 1) * gw // 16])
+                x_all[:, u * gw : (u + 1) * gw],
+                x_win[:].bitcast(U32).indirect(offs_t[:, u * gw // 16 : (u + 1) * gw // 16]),
             )
 
-        both = keep.tile([P, N], U32, name="w_codes", tag="x_then_w", align_bytes=64)
-        w_codes = [both[:, u * hw : (u + 1) * hw] for u in range(halves)]
-        quant_w(0)
-        quant_w(1)
+        w_codes = keep.tile([P, N], U32, name="w_codes", tag="x_then_woven", align_bytes=64)
+        quant_w(woven_early[:], 0, hw)
         chunks = S // CH
         first = [psum.tile([P, 2, CH], F32, name="first%d" % u, tag="first%d" % u) for u in range(2)]
-        scores = {c: psum.tile([P, PACK, CH], F32, name="scores%d" % c) for c in range(1, chunks)}
-        sums = {c: psum.tile([P, N // P, CH], F32, name="sums%d" % c) for c in range(chunks - 1)}
+        scores = {c: psum.tile([P, PACK, CH], F32, name="scores%d" % c, tag="scores%d" % c) for c in range(1, chunks)}
+        pair = [psum.tile([P, 2, 2 * CH], F32, name="pair%d" % h) for h in range(2)]
+        whole = psum.tile([P, N // P, CH], F32, name="whole")
+        last = []
 
         def slot(c, t):
             return first[t // 2][:, t % 2, :] if c == 0 else scores[c][:, t, :]
 
-        pos = [keep.tile([P, CH * PACK], F32, name="pos%d" % c, tag="pos%d" % c, align_bytes=64) for c in range(chunks - 1)]
-        z = [keep.tile([P, CH * PACK], BF16, name="z%d" % c, tag="z%d" % c, align_bytes=64) for c in range(chunks - 1)]
-        z.append(keep.tile([P, CH * PACK], BF16, name="z_last", tag="z_then_res", align_bytes=64))
+        pos = {}
+        z = {}
         z_codes = [keep.tile([P, CH], U32, name="z_codes%d" % c, align_bytes=64) for c in range(chunks)]
         z_scales = [keep.tile([P, CH], U8, name="z_scales%d" % c, align_bytes=64) for c in range(chunks)]
-        res = {c: keep.tile([P, N // P, CH], F32, name="res%d" % c, align_bytes=64) for c in range(chunks)}
         out_v = out.rearrange("(a p) j -> p a j", p=P)
 
         def score(c):
-            u, o = divmod(c * CH, gw)
             for t in range(PACK):
                 nc.tensor.matmul_mx(
                     out=slot(c, t),
                     lhsT=d_codes[:, t * P : (t + 1) * P].bitcast(FP8X4),
                     lhsT_scale=planes[:, t * P : (t + 1) * P],
-                    rhs=x_got[u][:, o : o + CH].bitcast(FP8X4),
+                    rhs=x_all[:, c * CH : (c + 1) * CH].bitcast(FP8X4),
                     rhs_scale=planes[:, H + c * CH : H + (c + 1) * CH],
                     start=True,
                     stop=True,
                 )
 
-        def positive(c):
-            if c in SCALAR_CHUNKS:
-                for t in range(PACK):
-                    if c == chunks - 1 and t < VECTOR_SLOTS:
-                        nc.vector.tensor_scalar(
-                            pos[c][:, t * CH : (t + 1) * CH], slot(c, t), 0.0, root[:, t : t + 1], ALU.max, ALU.mult
-                        )
-                    else:
-                        nc.scalar.activation(
-                            pos[c][:, t * CH : (t + 1) * CH], slot(c, t), ACT.Relu, scale=root[:, t : t + 1]
-                        )
-            else:
-                nc.vector.scalar_tensor_tensor(
-                    pos[c][:].rearrange("p (j t) -> p j t", t=PACK),
-                    scores[c][:].rearrange("p t j -> p j t"),
-                    0.0,
-                    root[:].unsqueeze(1).to_broadcast([P, CH, PACK]),
-                    ALU.max,
-                    ALU.mult,
-                )
+        def positive_scalar(c, tag):
+            pos[c] = keep.tile([P, CH * PACK], F32, name="pos%d" % c, tag=tag, align_bytes=64)
+            for t in range(PACK):
+                nc.scalar.activation(pos[c][:, t * CH : (t + 1) * CH], slot(c, t), ACT.Relu, scale=root[:, t : t + 1])
 
-        def square(c):
-            if c in SCALAR_CHUNKS:
+        def positive_vector(c, tag):
+            pos[c] = keep.tile([P, CH * PACK], F32, name="pos%d" % c, tag=tag, align_bytes=64)
+            nc.vector.scalar_tensor_tensor(
+                pos[c][:].rearrange("p (j t) -> p j t", t=PACK),
+                scores[c][:].rearrange("p t j -> p j t"),
+                0.0,
+                root[:].unsqueeze(1).to_broadcast([P, CH, PACK]),
+                ALU.max,
+                ALU.mult,
+            )
+
+        def square(c, weaves, tag):
+            z[c] = keep.tile([P, CH * PACK], BF16, name="z%d" % c, tag=tag, align_bytes=64)
+            if weaves:
                 nc.scalar.activation(
                     z[c][:].rearrange("p (c i t) -> p c t i", i=4, t=PACK),
                     pos[c][:].rearrange("p (t c i) -> p c t i", i=4, t=PACK),
@@ -176,11 +169,17 @@ def tile_picked_reluattn_relu_p_kernel(tc, x_words, x_scales, d_words, d_scales,
         def quant(c):
             nc.vector.quantize_mx(out=z_codes[c][:].bitcast(FP8X4), scales=z_scales[c][:], in_=z[c][:])
 
-        def value(c):
-            for a in range(N // P):
+        def value(c, blocks):
+            for a in blocks:
+                if c < 2:
+                    dst = pair[a // 2][:, a % 2, c * CH : (c + 1) * CH]
+                elif c == 2:
+                    dst = whole[:, a, :]
+                else:
+                    dst = last[a // 2][:, a % 2, :]
                 nc.tensor.matmul_mx(
-                    out=sums[c][:, a, :] if c < chunks - 1 else last[a // 2][:, a % 2, :],
-                    lhsT=w_codes[a // 2][:, a % 2 * P : (a % 2 + 1) * P].bitcast(FP8X4),
+                    out=dst,
+                    lhsT=w_codes[:, a * P : (a + 1) * P].bitcast(FP8X4),
                     lhsT_scale=w_scales[:, a * P : (a + 1) * P],
                     rhs=z_codes[c][:].bitcast(FP8X4),
                     rhs_scale=z_scales[c][:],
@@ -188,19 +187,22 @@ def tile_picked_reluattn_relu_p_kernel(tc, x_words, x_scales, d_words, d_scales,
                     stop=True,
                 )
 
-        def finish(c, a0, a1, queue):
-            cols = slice(c * CH, (c + 1) * CH)
+        def finish(sums, a0, a1, j0, j1, queue, tag):
+            res = keep.tile([P, a1 - a0, j1 - j0], F32, name="res_%d_%d" % (a0, j0), tag=tag, align_bytes=64)
             nc.vector.tensor_tensor(
-                res[c][:, a0:a1, :],
-                sums[c][:, a0:a1, :] if c < chunks - 1 else last[a0 // 2][:],
-                cnt_t[:, cols].unsqueeze(1).to_broadcast([P, a1 - a0, CH]),
-                ALU.mult,
+                res[:], sums, cnt_t[:, j0:j1].unsqueeze(1).to_broadcast([P, a1 - a0, j1 - j0]), ALU.mult
             )
-            queue.dma_start(out_v[:, a0:a1, cols], res[c][:, a0:a1, :])
+            queue.dma_start(out_v[:, a0:a1, j0:j1], res[:])
 
-        for a in range(2):
+        def weave_late(engine_copy, c0, c1):
+            engine_copy(
+                woven_late[:, c0:c1, :].rearrange("p (c i) t -> p c t i", i=4),
+                cast_late[:, :, c0:c1].rearrange("p t (c i) -> p c t i", i=4),
+            )
+
+        for h in range(2):
             nc.tensor.matmul_mx(
-                out=sums[a][:].rearrange("p a j -> p (a j)"),
+                out=pair[h][:].rearrange("p a j -> p (a j)"),
                 lhsT=d_got[:, 0:P].bitcast(FP8X4),
                 lhsT_scale=ds_got[:, 0:P],
                 rhs=d_got[:].bitcast(FP8X4),
@@ -208,44 +210,34 @@ def tile_picked_reluattn_relu_p_kernel(tc, x_words, x_scales, d_words, d_scales,
                 start=True,
                 stop=True,
             )
+        cnt_t = keep.tile([P, S], F32, name="cnt_t", tag="got_then_cnt", align_bytes=64)
+        nc.sync.dma_start(cnt_t[:], cnt)
         for c in range(chunks):
             score(c)
-        positive(0)
-        positive(1)
-        square(0)
-        positive(2)
-        square(1)
+        positive_scalar(0, "pos0")
+        positive_vector(1, "pos1")
+        square(0, True, "z0")
+        positive_vector(2, "pos2")
+        square(1, False, "z1")
         quant(0)
-        value(0)
-        pos.append(keep.tile([P, CH * PACK], F32, name="pos3", tag="pos0", align_bytes=64))
-        hq = CH // 2
-        nc.vector.scalar_tensor_tensor(
-            pos[3][:, 0 : hq * PACK].rearrange("p (j t) -> p j t", t=PACK),
-            scores[3][:, :, 0:hq].rearrange("p t j -> p j t"),
-            0.0,
-            root[:].unsqueeze(1).to_broadcast([P, hq, PACK]),
-            ALU.max,
-            ALU.mult,
-        )
-        pos_s = keep.tile([P, PACK, hq], F32, name="pos_s", tag="z0", align_bytes=64)
-        for t in range(PACK):
-            nc.scalar.activation(pos_s[:, t, :], scores[3][:, t, hq:CH], ACT.Relu, scale=root[:, t : t + 1])
-        square(2)
+        value(0, (0, 1))
+        woven_late = keep.tile([P, hw, PACK], BF16, name="woven_late", tag="pos0", align_bytes=64)
+        weave_late(nc.vector.tensor_copy, 0, hw)
         quant(1)
-        value(1)
-        nc.scalar.activation(
-            z[3][:, hq * PACK :].rearrange("p (c i t) -> p c t i", i=4, t=PACK),
-            pos_s[:].rearrange("p t (c i) -> p c t i", i=4),
-            ACT.Square,
-        )
-        nc.scalar.activation(z[3][:, 0 : hq * PACK], pos[3][:, 0 : hq * PACK], ACT.Square)
-        finish(0, 0, 4, nc.sync)
+        value(1, (0, 1))
+        quant_w(woven_late[:], hw, N)
+        value(0, (2, 3))
+        value(1, (2, 3))
+        square(2, False, "z2")
+        positive_scalar(3, "z0")
         quant(2)
-        value(2)
-        finish(1, 0, 4, nc.sync)
+        value(2, range(4))
+        square(3, True, "z3")
+        finish(pair[0][:], 0, 2, 0, 2 * CH, nc.sync, "r0")
         quant(3)
-        last = [psum.tile([P, 2, CH], F32, name="last%d" % u, tag="first%d" % u) for u in range(2)]
-        value(3)
-        finish(2, 0, 4, nc.scalar)
-        finish(3, 0, 2, nc.sync)
-        finish(3, 2, 4, nc.scalar)
+        last.extend(psum.tile([P, 2, CH], F32, name="last%d" % u, tag="first%d" % u) for u in range(2))
+        value(3, range(4))
+        finish(pair[1][:], 2, 4, 0, 2 * CH, nc.sync, "r1")
+        finish(whole[:], 0, 4, 2 * CH, 3 * CH, nc.scalar, "r2")
+        finish(last[0][:], 0, 2, 3 * CH, 4 * CH, nc.sync, "r3")
+        finish(last[1][:], 2, 4, 3 * CH, 4 * CH, nc.scalar, "r4")

@@ -33,23 +33,20 @@ def tile_picked_reluattn_relu_p_kernel(tc, x_words, x_scales, d_words, d_scales,
         x_win = keep.tile([P, T], I32, name="x_win", tag="x_then_woven", align_bytes=64)
         gn_t = keep.tile([P, PACK], F32, name="gn_t")
         hw = N // 2
-        w_raw = [keep.tile([P, 2, hw], F32, name="w_raw%d" % u, align_bytes=64) for u in range(2)]
+        w_raw = [keep.tile([P, n, hw], F32, name="w_raw%d" % n, tag="w_raw%d" % n, align_bytes=64) for n in (3, 1)]
 
-        for win in (ds_win, xs_win):
-            nc.vector.memset(win[:, 0:1024].bitcast(I32), 0)
-            nc.gpsimd.memset(win[:, 1024:2048].bitcast(I32), 0)
+        nc.vector.memset(ds_win[:].bitcast(I32), 0)
+        nc.gpsimd.memset(xs_win[:].bitcast(I32), 0)
         w_rows = w1.rearrange("(p t) m -> p t m", t=PACK)
         nc.scalar.dma_start(gn_t[:], gn.rearrange("(p t) o -> p (t o)", t=PACK))
-        nc.scalar.dma_start(w_raw[0][:], w_rows[:, 0:2, 0:hw])
+        nc.scalar.dma_start(w_raw[0][:], w_rows[:, 0:3, 0:hw])
         nc.sync.dma_start(kidx_t[:], kidx)
         nc.sync.dma_start(offs_t[:], offs)
         nc.sync.dma_start(ds_win[0:P:8, :].bitcast(I32), d_scales[0].bitcast(I32))
         nc.sync.dma_start(xs_win[0:P:8, :].bitcast(I32), x_scales[0].bitcast(I32))
-        nc.sync.dma_start(w_raw[1][:], w_rows[:, 2:4, 0:hw])
+        nc.sync.dma_start(w_raw[1][:], w_rows[:, 3:4, 0:hw])
         nc.sync.dma_start(d_win[:], d_words[0].rearrange("p n t -> p (n t)").bitcast(I32))
         nc.sync.dma_start(x_win[:], x_words[0].rearrange("p n t -> p (n t)").bitcast(I32))
-        w_late = [keep.tile([P, 2, hw], F32, name="w_late0", align_bytes=64)]
-        nc.sync.dma_start(w_late[0][:], w_rows[:, 0:2, hw:N])
 
         sign = keep.tile([P, PACK], F32, name="sign")
         mag = keep.tile([P, PACK], F32, name="mag")
@@ -62,7 +59,7 @@ def tile_picked_reluattn_relu_p_kernel(tc, x_words, x_scales, d_words, d_scales,
         cast_early = keep.tile([P, PACK, hw], BF16, name="cast_early", align_bytes=64)
         woven_early = keep.tile([P, hw, PACK], BF16, name="woven_early", align_bytes=64)
         for t in range(PACK):
-            nc.scalar.activation(cast_early[:, t, :], w_raw[t // 2][:, t % 2, :], ACT.Copy, scale=sign[:, t : t + 1])
+            nc.scalar.activation(cast_early[:, t, :], w_raw[t // 3][:, t % 3, :], ACT.Copy, scale=sign[:, t : t + 1])
         nc.scalar.copy(
             woven_early[:].rearrange("p (c i) t -> p c t i", i=4),
             cast_early[:].rearrange("p t (c i) -> p c t i", i=4),
@@ -70,21 +67,22 @@ def tile_picked_reluattn_relu_p_kernel(tc, x_words, x_scales, d_words, d_scales,
 
         ds_got = keep.tile([P, H], U8, name="ds_got", align_bytes=64)
         xs_got = keep.tile([P, S], U8, name="xs_got", tag="xs_then_w", align_bytes=64)
-        planes = keep.tile([P, H + S], U8, name="planes", align_bytes=64)
+        planes = keep.tile([P, H + S], U8, name="planes", tag="w_raw3", align_bytes=64)
         nc.vector.tensor_copy(ds_got[:], ds_win[:].indirect(kidx_t[:]))
         nc.vector.tensor_copy(xs_got[:], xs_win[:].indirect(offs_t[:]))
         nc.vector.tensor_copy(
-            planes[:, 0:H].rearrange("p (t m) -> p m t", t=PACK),
-            ds_got[:].rearrange("p (m t) -> p m t", t=PACK),
+            planes[:, 0:H].rearrange("p (t m) -> p t m", t=PACK),
+            ds_got[:].rearrange("p (m t) -> p t m", t=PACK),
         )
         nc.vector.tensor_copy(planes[:, H : H + S].bitcast(I32), xs_got[:].bitcast(I32))
         for r in range(1, 4):
             nc.sync.dma_start(planes[r:P:32, :].bitcast(I32), planes[8 * r : P : 32, :].bitcast(I32))
-        w_late.append(keep.tile([P, 2, hw], F32, name="w_late1", tag="xs_then_w", align_bytes=64))
-        nc.sync.dma_start(w_late[1][:], w_rows[:, 2:4, hw:N])
+        w_late = keep.tile([P, PACK, hw], F32, name="w_late", tag="xs_then_w", align_bytes=64)
+        for u in range(2):
+            nc.sync.dma_start(w_late[:, 2 * u : 2 * u + 2, :], w_rows[:, 2 * u : 2 * u + 2, hw:N])
         cast_late = keep.tile([P, PACK, hw], BF16, name="cast_late", align_bytes=64)
         for t in range(PACK):
-            nc.gpsimd.tensor_scalar(cast_late[:, t, :], w_late[t // 2][:, t % 2, :], sign[:, t : t + 1], 0.0, ALU.mult, ALU.add)
+            nc.gpsimd.tensor_scalar(cast_late[:, t, :], w_late[:, t, :], sign[:, t : t + 1], 0.0, ALU.mult, ALU.add)
 
         def quant_w(woven, c0, c1):
             nc.vector.quantize_mx(
@@ -95,11 +93,15 @@ def tile_picked_reluattn_relu_p_kernel(tc, x_words, x_scales, d_words, d_scales,
 
         d_codes = keep.tile([P, H], U32, name="d_codes", align_bytes=64)
         d_got = keep.tile([P, H], U32, name="d_got", tag="got_then_cnt", align_bytes=64)
-        nc.vector.tensor_copy(d_got[:], d_win[:].bitcast(U32).indirect(kidx_t[:]))
-        nc.vector.tensor_copy(
-            d_codes[:].rearrange("p (t m) -> p m t", t=PACK),
-            d_got[:].rearrange("p (m t) -> p m t", t=PACK),
-        )
+        for u in range(2):
+            nc.vector.tensor_copy(
+                d_got[:, u * 256 : (u + 1) * 256], d_win[:].bitcast(U32).indirect(kidx_t[:, u * 16 : (u + 1) * 16])
+            )
+        for u in range(2):
+            nc.vector.tensor_copy(
+                d_codes[:].rearrange("p (t m) -> p m t", t=PACK)[:, u * 64 : (u + 1) * 64, :],
+                d_got[:, u * 256 : (u + 1) * 256].rearrange("p (m t) -> p m t", t=PACK),
+            )
 
         gw = 256
         x_all = keep.tile([P, S], U32, name="x_all", align_bytes=64)

@@ -36,17 +36,20 @@ def tile_picked_reluattn_relu_p_kernel(tc, x_words, x_scales, d_words, d_scales,
         w_raw = [keep.tile([P, n, hw], F32, name="w_raw%d" % n, tag="w_raw%d" % n, align_bytes=64) for n in (3, 1)]
 
         nc.vector.memset(ds_win[:].bitcast(I32), 0)
-        nc.gpsimd.memset(xs_win[:].bitcast(I32), 0)
+        nc.vector.memset(xs_win[:].bitcast(I32), 0)
         w_rows = w1.rearrange("(p t) m -> p t m", t=PACK)
         nc.scalar.dma_start(gn_t[:], gn.rearrange("(p t) o -> p (t o)", t=PACK))
         nc.scalar.dma_start(w_raw[0][:], w_rows[:, 0:3, 0:hw])
         nc.sync.dma_start(kidx_t[:], kidx)
         nc.sync.dma_start(offs_t[:], offs)
         nc.sync.dma_start(ds_win[0:P:8, :].bitcast(I32), d_scales[0].bitcast(I32))
-        nc.sync.dma_start(xs_win[0:P:8, :].bitcast(I32), x_scales[0].bitcast(I32))
         nc.sync.dma_start(w_raw[1][:], w_rows[:, 3:4, 0:hw])
+        nc.sync.dma_start(xs_win[0:P:8, :].bitcast(I32), x_scales[0].bitcast(I32))
         nc.sync.dma_start(d_win[:], d_words[0].rearrange("p n t -> p (n t)").bitcast(I32))
         nc.sync.dma_start(x_win[:], x_words[0].rearrange("p n t -> p (n t)").bitcast(I32))
+
+        w_late = [keep.tile([P, 2, hw], F32, name="w_late0", align_bytes=64)]
+        nc.sync.dma_start(w_late[0][:], w_rows[:, 0:2, hw:N])
 
         sign = keep.tile([P, PACK], F32, name="sign")
         mag = keep.tile([P, PACK], F32, name="mag")
@@ -77,12 +80,11 @@ def tile_picked_reluattn_relu_p_kernel(tc, x_words, x_scales, d_words, d_scales,
         nc.vector.tensor_copy(planes[:, H : H + S].bitcast(I32), xs_got[:].bitcast(I32))
         for r in range(1, 4):
             nc.sync.dma_start(planes[r:P:32, :].bitcast(I32), planes[8 * r : P : 32, :].bitcast(I32))
-        w_late = keep.tile([P, PACK, hw], F32, name="w_late", tag="xs_then_w", align_bytes=64)
-        for u in range(2):
-            nc.sync.dma_start(w_late[:, 2 * u : 2 * u + 2, :], w_rows[:, 2 * u : 2 * u + 2, hw:N])
+        w_late.append(keep.tile([P, 2, hw], F32, name="w_late1", tag="xs_then_w", align_bytes=64))
+        nc.sync.dma_start(w_late[1][:], w_rows[:, 2:4, hw:N])
         cast_late = keep.tile([P, PACK, hw], BF16, name="cast_late", align_bytes=64)
         for t in range(PACK):
-            nc.gpsimd.tensor_scalar(cast_late[:, t, :], w_late[:, t, :], sign[:, t : t + 1], 0.0, ALU.mult, ALU.add)
+            nc.gpsimd.tensor_scalar(cast_late[:, t, :], w_late[t // 2][:, t % 2, :], sign[:, t : t + 1], 0.0, ALU.mult, ALU.add)
 
         def quant_w(woven, c0, c1):
             nc.vector.quantize_mx(

@@ -38,7 +38,7 @@ def tile_picked_reluattn_relu_p_kernel(tc, x_words, x_scales, d_words, d_scales,
         nc.vector.memset(ds_win[:].bitcast(I32), 0)
         nc.vector.memset(xs_win[:].bitcast(I32), 0)
         w_rows = w1.rearrange("(p t) m -> p t m", t=PACK)
-        nc.scalar.dma_start(gn_t[:], gn.rearrange("(p t) o -> p (t o)", t=PACK))
+        nc.sync.dma_start(gn_t[:], gn.rearrange("(p t) o -> p (t o)", t=PACK))
         nc.scalar.dma_start(w_raw[0][:], w_rows[:, 0:3, 0:hw])
         nc.sync.dma_start(kidx_t[:], kidx)
         nc.sync.dma_start(offs_t[:], offs)
@@ -47,9 +47,6 @@ def tile_picked_reluattn_relu_p_kernel(tc, x_words, x_scales, d_words, d_scales,
         nc.sync.dma_start(xs_win[0:P:8, :].bitcast(I32), x_scales[0].bitcast(I32))
         nc.sync.dma_start(d_win[:], d_words[0].rearrange("p n t -> p (n t)").bitcast(I32))
         nc.sync.dma_start(x_win[:], x_words[0].rearrange("p n t -> p (n t)").bitcast(I32))
-
-        w_late = [keep.tile([P, 2, hw], F32, name="w_late0", align_bytes=64)]
-        nc.sync.dma_start(w_late[0][:], w_rows[:, 0:2, hw:N])
 
         sign = keep.tile([P, PACK], F32, name="sign")
         mag = keep.tile([P, PACK], F32, name="mag")
@@ -80,11 +77,12 @@ def tile_picked_reluattn_relu_p_kernel(tc, x_words, x_scales, d_words, d_scales,
         nc.vector.tensor_copy(planes[:, H : H + S].bitcast(I32), xs_got[:].bitcast(I32))
         for r in range(1, 4):
             nc.sync.dma_start(planes[r:P:32, :].bitcast(I32), planes[8 * r : P : 32, :].bitcast(I32))
-        w_late.append(keep.tile([P, 2, hw], F32, name="w_late1", tag="xs_then_w", align_bytes=64))
-        nc.sync.dma_start(w_late[1][:], w_rows[:, 2:4, hw:N])
+        w_late = keep.tile([P, PACK, hw], F32, name="w_late", tag="xs_then_w", align_bytes=64)
+        for u in range(2):
+            nc.sync.dma_start(w_late[:, 2 * u : 2 * u + 2, :], w_rows[:, 2 * u : 2 * u + 2, hw:N])
         cast_late = keep.tile([P, PACK, hw], BF16, name="cast_late", align_bytes=64)
         for t in range(PACK):
-            nc.gpsimd.tensor_scalar(cast_late[:, t, :], w_late[t // 2][:, t % 2, :], sign[:, t : t + 1], 0.0, ALU.mult, ALU.add)
+            nc.gpsimd.tensor_scalar(cast_late[:, t, :], w_late[:, t, :], sign[:, t : t + 1], 0.0, ALU.mult, ALU.add)
 
         def quant_w(woven, c0, c1):
             nc.vector.quantize_mx(
@@ -119,10 +117,13 @@ def tile_picked_reluattn_relu_p_kernel(tc, x_words, x_scales, d_words, d_scales,
         first = [psum.tile([P, 2, CH], F32, name="first%d" % u, tag="first%d" % u) for u in range(2)]
         scores = {c: psum.tile([P, PACK, CH], F32, name="scores%d" % c, tag="scores%d" % c) for c in range(1, chunks)}
         pair = [psum.tile([P, 2, 2 * CH], F32, name="pair%d" % h) for h in range(2)]
-        whole = psum.tile([P, N // P, CH], F32, name="whole")
+        very_first = psum.tile([P, CH], F32, name="very_first", tag="whole")
+        whole = []
         last = []
 
         def slot(c, t):
+            if (c, t) == (0, 0):
+                return very_first[:]
             return first[t // 2][:, t % 2, :] if c == 0 else scores[c][:, t, :]
 
         pos = {}
@@ -178,7 +179,7 @@ def tile_picked_reluattn_relu_p_kernel(tc, x_words, x_scales, d_words, d_scales,
                 if c < 2:
                     dst = pair[a // 2][:, a % 2, c * CH : (c + 1) * CH]
                 elif c == 2:
-                    dst = whole[:, a, :]
+                    dst = whole[0][:, a, :]
                 else:
                     dst = last[a // 2][:, a % 2, :]
                 nc.tensor.matmul_mx(
@@ -235,6 +236,7 @@ def tile_picked_reluattn_relu_p_kernel(tc, x_words, x_scales, d_words, d_scales,
         square(2, False, "z2")
         positive_scalar(3, "z0")
         quant(2)
+        whole.append(psum.tile([P, N // P, CH], F32, name="whole", tag="whole"))
         value(2, range(4))
         square(3, True, "z3")
         finish(pair[0][:], 0, 2, 0, 2 * CH, nc.sync, "r0")
@@ -242,6 +244,6 @@ def tile_picked_reluattn_relu_p_kernel(tc, x_words, x_scales, d_words, d_scales,
         last.extend(psum.tile([P, 2, CH], F32, name="last%d" % u, tag="first%d" % u) for u in range(2))
         value(3, range(4))
         finish(pair[1][:], 2, 4, 0, 2 * CH, nc.sync, "r1")
-        finish(whole[:], 0, 4, 2 * CH, 3 * CH, nc.scalar, "r2")
+        finish(whole[0][:], 0, 4, 2 * CH, 3 * CH, nc.scalar, "r2")
         finish(last[0][:], 0, 2, 3 * CH, 4 * CH, nc.sync, "r3")
         finish(last[1][:], 2, 4, 3 * CH, 4 * CH, nc.scalar, "r4")

@@ -48,6 +48,9 @@ def tile_picked_reluattn_relu_p_kernel(tc, x_words, x_scales, d_words, d_scales,
         nc.sync.dma_start(d_win[:], d_words[0].rearrange("p n t -> p (n t)").bitcast(I32))
         nc.sync.dma_start(x_win[:], x_words[0].rearrange("p n t -> p (n t)").bitcast(I32))
 
+        w_late = [keep.tile([P, 2, hw], F32, name="w_late0", align_bytes=64)]
+        nc.sync.dma_start(w_late[0][:], w_rows[:, 0:2, hw:N])
+
         sign = keep.tile([P, PACK], F32, name="sign")
         mag = keep.tile([P, PACK], F32, name="mag")
         root = keep.tile([P, PACK], F32, name="root")
@@ -77,12 +80,11 @@ def tile_picked_reluattn_relu_p_kernel(tc, x_words, x_scales, d_words, d_scales,
         nc.vector.tensor_copy(planes[:, H : H + S].bitcast(I32), xs_got[:].bitcast(I32))
         for r in range(1, 4):
             nc.sync.dma_start(planes[r:P:32, :].bitcast(I32), planes[8 * r : P : 32, :].bitcast(I32))
-        w_late = keep.tile([P, PACK, hw], F32, name="w_late", tag="xs_then_w", align_bytes=64)
-        for u in range(2):
-            nc.sync.dma_start(w_late[:, 2 * u : 2 * u + 2, :], w_rows[:, 2 * u : 2 * u + 2, hw:N])
+        w_late.append(keep.tile([P, 2, hw], F32, name="w_late1", tag="xs_then_w", align_bytes=64))
+        nc.sync.dma_start(w_late[1][:], w_rows[:, 2:4, hw:N])
         cast_late = keep.tile([P, PACK, hw], BF16, name="cast_late", align_bytes=64)
         for t in range(PACK):
-            nc.gpsimd.tensor_scalar(cast_late[:, t, :], w_late[:, t, :], sign[:, t : t + 1], 0.0, ALU.mult, ALU.add)
+            nc.gpsimd.tensor_scalar(cast_late[:, t, :], w_late[t // 2][:, t % 2, :], sign[:, t : t + 1], 0.0, ALU.mult, ALU.add)
 
         def quant_w(woven, c0, c1):
             nc.vector.quantize_mx(
@@ -115,8 +117,9 @@ def tile_picked_reluattn_relu_p_kernel(tc, x_words, x_scales, d_words, d_scales,
         quant_w(woven_early[:], 0, hw)
         chunks = S // CH
         first = [psum.tile([P, 2, CH], F32, name="first%d" % u, tag="first%d" % u) for u in range(2)]
-        scores = {c: psum.tile([P, PACK, CH], F32, name="scores%d" % c, tag="scores%d" % c) for c in range(1, chunks)}
-        pair = [psum.tile([P, 2, 2 * CH], F32, name="pair%d" % h) for h in range(2)]
+        scores = {c: psum.tile([P, PACK, CH], F32, name="scores%d" % c, tag="scores%d" % c) for c in (1, 3)}
+        third = {1: psum.tile([P, 2, CH], F32, name="third1", tag="third1")}
+        pair = [psum.tile([P, 2, 2 * CH], F32, name="pair0")]
         very_first = psum.tile([P, CH], F32, name="very_first", tag="whole")
         whole = []
         last = []
@@ -124,7 +127,9 @@ def tile_picked_reluattn_relu_p_kernel(tc, x_words, x_scales, d_words, d_scales,
         def slot(c, t):
             if (c, t) == (0, 0):
                 return very_first[:]
-            return first[t // 2][:, t % 2, :] if c == 0 else scores[c][:, t, :]
+            if c in scores:
+                return scores[c][:, t, :]
+            return (first if c == 0 else third)[t // 2][:, t % 2, :]
 
         pos = {}
         z = {}
@@ -132,8 +137,8 @@ def tile_picked_reluattn_relu_p_kernel(tc, x_words, x_scales, d_words, d_scales,
         z_scales = [keep.tile([P, CH], U8, name="z_scales%d" % c, align_bytes=64) for c in range(chunks)]
         out_v = out.rearrange("(a p) j -> p a j", p=P)
 
-        def score(c):
-            for t in range(PACK):
+        def score(c, slots):
+            for t in slots:
                 nc.tensor.matmul_mx(
                     out=slot(c, t),
                     lhsT=d_codes[:, t * P : (t + 1) * P].bitcast(FP8X4),
@@ -159,6 +164,19 @@ def tile_picked_reluattn_relu_p_kernel(tc, x_words, x_scales, d_words, d_scales,
                 ALU.max,
                 ALU.mult,
             )
+
+        def positive_shared(c, tag):
+            pos[c] = keep.tile([P, CH * PACK], F32, name="pos%d" % c, tag=tag, align_bytes=64)
+            nc.vector.scalar_tensor_tensor(
+                pos[c][:, 2 * CH : 4 * CH].rearrange("p (t j) -> p t j", t=2),
+                third[1][:],
+                0.0,
+                root[:, 2:4].unsqueeze(2).to_broadcast([P, 2, CH]),
+                ALU.max,
+                ALU.mult,
+            )
+            for t in range(2):
+                nc.scalar.activation(pos[c][:, t * CH : (t + 1) * CH], slot(c, t), ACT.Relu, scale=root[:, t : t + 1])
 
         def square(c, weaves, tag):
             z[c] = keep.tile([P, CH * PACK], BF16, name="z%d" % c, tag=tag, align_bytes=64)
@@ -207,7 +225,7 @@ def tile_picked_reluattn_relu_p_kernel(tc, x_words, x_scales, d_words, d_scales,
 
         for h in range(2):
             nc.tensor.matmul_mx(
-                out=pair[h][:].rearrange("p a j -> p (a j)"),
+                out=scores[2 * h + 1][:].rearrange("p a j -> p (a j)"),
                 lhsT=d_got[:, 0:P].bitcast(FP8X4),
                 lhsT_scale=ds_got[:, 0:P],
                 rhs=d_got[:].bitcast(FP8X4),
@@ -218,12 +236,14 @@ def tile_picked_reluattn_relu_p_kernel(tc, x_words, x_scales, d_words, d_scales,
         cnt_t = keep.tile([P, S], F32, name="cnt_t", tag="got_then_cnt", align_bytes=64)
         nc.sync.dma_start(cnt_t[:], cnt)
         for c in range(chunks):
-            score(c)
+            score(c, (2, 3) if c == 2 else range(PACK))
         positive_scalar(0, "pos0")
+        third[0] = psum.tile([P, 2, CH], F32, name="third0", tag="first1")
+        score(2, (0, 1))
         positive_vector(1, "pos1")
         square(0, True, "z0")
-        positive_vector(2, "pos2")
         square(1, False, "z1")
+        positive_shared(2, "pos2")
         quant(0)
         value(0, (0, 1))
         woven_late = keep.tile([P, hw, PACK], BF16, name="woven_late", tag="pos0", align_bytes=64)
@@ -231,19 +251,20 @@ def tile_picked_reluattn_relu_p_kernel(tc, x_words, x_scales, d_words, d_scales,
         quant(1)
         value(1, (0, 1))
         quant_w(woven_late[:], hw, N)
+        pair.append(psum.tile([P, 2, 2 * CH], F32, name="pair1", tag="third1"))
         value(0, (2, 3))
         value(1, (2, 3))
-        square(2, False, "z2")
+        square(2, True, "z2")
         positive_scalar(3, "z0")
+        finish(pair[0][:], 0, 2, 0, 2 * CH, nc.sync, "r0")
         quant(2)
         whole.append(psum.tile([P, N // P, CH], F32, name="whole", tag="whole"))
         value(2, range(4))
         square(3, True, "z3")
-        finish(pair[0][:], 0, 2, 0, 2 * CH, nc.sync, "r0")
+        finish(pair[1][:], 2, 4, 0, 2 * CH, nc.sync, "r1")
         quant(3)
         last.extend(psum.tile([P, 2, CH], F32, name="last%d" % u, tag="first%d" % u) for u in range(2))
         value(3, range(4))
-        finish(pair[1][:], 2, 4, 0, 2 * CH, nc.sync, "r1")
-        finish(whole[0][:], 0, 4, 2 * CH, 3 * CH, nc.scalar, "r2")
+        finish(whole[0][:], 0, 4, 2 * CH, 3 * CH, nc.scalar, "z0")
         finish(last[0][:], 0, 2, 3 * CH, 4 * CH, nc.sync, "r3")
         finish(last[1][:], 2, 4, 3 * CH, 4 * CH, nc.scalar, "r4")

@@ -16,6 +16,7 @@ K, T, S, N, G, H = 512, 2048, 512, 512, 2048, 512
 P = 128
 PACK = 4
 CH = 128
+HALF = N // 2
 FLOPS = 2 * K * H * S + 2 * H * N * S
 
 
@@ -25,52 +26,58 @@ def tile_picked_reluattn_relu_p_kernel(tc, x_words, x_scales, d_words, d_scales,
         keep = ctx.enter_context(tc.tile_pool(name="keep", bufs=1))
         psum = ctx.enter_context(tc.psum_pool(name="psum", bufs=1))
 
+        def sb(shape, dtype, name, tag=None):
+            return keep.tile(shape, dtype, name=name, tag=tag or name, align_bytes=64)
+
+        def bank(shape, name, tag):
+            return psum.tile(shape, F32, name=name, tag=tag)
+
         kidx_t = keep.tile([P, H // 16], U16, name="kidx_t")
         offs_t = keep.tile([P, S // 16], U16, name="offs_t")
-        ds_win = keep.tile([P, G], U8, name="ds_win", align_bytes=64)
-        xs_win = keep.tile([P, T], U8, name="xs_win", align_bytes=64)
-        d_win = keep.tile([P, G], I32, name="d_win", tag="d_then_cnt", align_bytes=64)
-        x_win = keep.tile([P, T], I32, name="x_win", tag="x_then_woven", align_bytes=64)
-        gn_t = keep.tile([P, PACK], F32, name="gn_t")
-        hw = N // 2
-        w_raw = [keep.tile([P, n, hw], F32, name="w_raw%d" % n, tag="w_raw%d" % n, align_bytes=64) for n in (3, 1)]
+        ds_win = sb([P, G], U8, "ds_win")
+        xs_win = sb([P, T], U8, "xs_win")
+        d_win = sb([P, G], I32, "d_win")
+        x_win = sb([P, T], I32, "x_win", "x_then_w")
+        gn_t = sb([P, PACK], F32, "gn_t")
+        w_early = [sb([P, n, HALF], F32, "w_early%d" % n) for n in (3, 1)]
 
         nc.vector.memset(ds_win[:].bitcast(I32), 0)
         nc.vector.memset(xs_win[:].bitcast(I32), 0)
         w_rows = w1.rearrange("(p t) m -> p t m", t=PACK)
         nc.sync.dma_start(gn_t[:], gn.rearrange("(p t) o -> p (t o)", t=PACK))
-        nc.scalar.dma_start(w_raw[0][:], w_rows[:, 0:3, 0:hw])
+        nc.scalar.dma_start(w_early[0][:], w_rows[:, 0:3, 0:HALF])
         nc.sync.dma_start(kidx_t[:], kidx)
         nc.sync.dma_start(offs_t[:], offs)
         nc.sync.dma_start(ds_win[0:P:8, :].bitcast(I32), d_scales[0].bitcast(I32))
-        nc.sync.dma_start(w_raw[1][:], w_rows[:, 3:4, 0:hw])
+        nc.sync.dma_start(w_early[1][:], w_rows[:, 3:4, 0:HALF])
         nc.sync.dma_start(xs_win[0:P:8, :].bitcast(I32), x_scales[0].bitcast(I32))
         nc.sync.dma_start(d_win[:], d_words[0].rearrange("p n t -> p (n t)").bitcast(I32))
         nc.sync.dma_start(x_win[:], x_words[0].rearrange("p n t -> p (n t)").bitcast(I32))
+        w_late = [sb([P, 2, HALF], F32, "w_late0")]
+        nc.sync.dma_start(w_late[0][:], w_rows[:, 0:2, HALF:N])
 
-        w_late = [keep.tile([P, 2, hw], F32, name="w_late0", align_bytes=64)]
-        nc.sync.dma_start(w_late[0][:], w_rows[:, 0:2, hw:N])
-
-        sign = keep.tile([P, PACK], F32, name="sign")
-        mag = keep.tile([P, PACK], F32, name="mag")
-        root = keep.tile([P, PACK], F32, name="root")
+        sign = sb([P, PACK], F32, "sign")
+        mag = sb([P, PACK], F32, "mag")
+        root = sb([P, PACK], F32, "root")
         nc.vector.scalar_tensor_tensor(mag[:], gn_t[:], -1.0, gn_t[:], ALU.mult, ALU.max)
         nc.vector.tensor_scalar(sign[:], gn_t[:], 0.0, 0.5, ALU.is_ge, ALU.subtract)
         nc.scalar.activation(root[:], mag[:], ACT.Sqrt, scale=2.0 * 0.0625 * 0.0625)
 
-        w_scales = keep.tile([P, N], U8, name="w_scales", align_bytes=64)
-        cast_early = keep.tile([P, PACK, hw], BF16, name="cast_early", align_bytes=64)
-        woven_early = keep.tile([P, hw, PACK], BF16, name="woven_early", align_bytes=64)
-        for t in range(PACK):
-            nc.scalar.activation(cast_early[:, t, :], w_raw[t // 3][:, t % 3, :], ACT.Copy, scale=sign[:, t : t + 1])
-        nc.scalar.copy(
-            woven_early[:].rearrange("p (c i) t -> p c t i", i=4),
-            cast_early[:].rearrange("p t (c i) -> p c t i", i=4),
-        )
+        def weave(copy, woven, cast):
+            copy(
+                woven.rearrange("p (c i) t -> p c t i", i=4),
+                cast.rearrange("p t (c i) -> p c t i", i=4),
+            )
 
-        ds_got = keep.tile([P, H], U8, name="ds_got", align_bytes=64)
-        xs_got = keep.tile([P, S], U8, name="xs_got", tag="xs_then_w", align_bytes=64)
-        planes = keep.tile([P, H + S], U8, name="planes", tag="w_raw3", align_bytes=64)
+        cast_early = sb([P, PACK, HALF], BF16, "cast_early")
+        woven_early = sb([P, HALF, PACK], BF16, "woven_early")
+        for t in range(PACK):
+            nc.scalar.activation(cast_early[:, t, :], w_early[t // 3][:, t % 3, :], ACT.Copy, scale=sign[:, t : t + 1])
+        weave(nc.scalar.copy, woven_early[:], cast_early[:])
+
+        ds_got = sb([P, H], U8, "ds_got")
+        xs_got = sb([P, S], U8, "xs_got", "xs_then_w")
+        planes = sb([P, H + S], U8, "planes", "w_early3")
         nc.vector.tensor_copy(ds_got[:], ds_win[:].indirect(kidx_t[:]))
         nc.vector.tensor_copy(xs_got[:], xs_win[:].indirect(offs_t[:]))
         nc.vector.tensor_copy(
@@ -80,21 +87,14 @@ def tile_picked_reluattn_relu_p_kernel(tc, x_words, x_scales, d_words, d_scales,
         nc.vector.tensor_copy(planes[:, H : H + S].bitcast(I32), xs_got[:].bitcast(I32))
         for r in range(1, 4):
             nc.sync.dma_start(planes[r:P:32, :].bitcast(I32), planes[8 * r : P : 32, :].bitcast(I32))
-        w_late.append(keep.tile([P, 2, hw], F32, name="w_late1", tag="xs_then_w", align_bytes=64))
-        nc.sync.dma_start(w_late[1][:], w_rows[:, 2:4, hw:N])
-        cast_late = keep.tile([P, PACK, hw], BF16, name="cast_late", align_bytes=64)
+        w_late.append(sb([P, 2, HALF], F32, "w_late1", "xs_then_w"))
+        nc.sync.dma_start(w_late[1][:], w_rows[:, 2:4, HALF:N])
+        cast_late = sb([P, PACK, HALF], BF16, "cast_late")
         for t in range(PACK):
             nc.gpsimd.tensor_scalar(cast_late[:, t, :], w_late[t // 2][:, t % 2, :], sign[:, t : t + 1], 0.0, ALU.mult, ALU.add)
 
-        def quant_w(woven, c0, c1):
-            nc.vector.quantize_mx(
-                out=w_codes[:, c0:c1].bitcast(FP8X4),
-                scales=w_scales[:, c0:c1],
-                in_=woven.rearrange("p m t -> p (m t)"),
-            )
-
-        d_codes = keep.tile([P, H], U32, name="d_codes", align_bytes=64)
-        d_got = keep.tile([P, H], U32, name="d_got", tag="got_then_cnt", align_bytes=64)
+        d_got = sb([P, H], U32, "d_got", "got_then_cnt")
+        d_codes = sb([P, H], U32, "d_codes")
         for u in range(2):
             nc.vector.tensor_copy(
                 d_got[:, u * 256 : (u + 1) * 256], d_win[:].bitcast(U32).indirect(kidx_t[:, u * 16 : (u + 1) * 16])
@@ -104,167 +104,137 @@ def tile_picked_reluattn_relu_p_kernel(tc, x_words, x_scales, d_words, d_scales,
                 d_codes[:].rearrange("p (t m) -> p m t", t=PACK)[:, u * 64 : (u + 1) * 64, :],
                 d_got[:, u * 256 : (u + 1) * 256].rearrange("p (m t) -> p m t", t=PACK),
             )
+        cnt_t = sb([P, S], F32, "cnt_t", "got_then_cnt")
+        nc.sync.dma_start(cnt_t[:], cnt)
 
-        gw = 256
-        x_all = keep.tile([P, S], U32, name="x_all", align_bytes=64)
-        for u in range(S // gw):
-            nc.vector.tensor_copy(
-                x_all[:, u * gw : (u + 1) * gw],
-                x_win[:].bitcast(U32).indirect(offs_t[:, u * gw // 16 : (u + 1) * gw // 16]),
+        x_got = sb([P, S], U32, "x_got")
+        for j0, j1 in ((0, 128), (128, 256), (256, 512)):
+            nc.vector.tensor_copy(x_got[:, j0:j1], x_win[:].bitcast(U32).indirect(offs_t[:, j0 // 16 : j1 // 16]))
+
+        w_codes = sb([P, N], U32, "w_codes", "x_then_w")
+        w_scales = sb([P, N], U8, "w_scales")
+
+        def quant_w(woven, c0, c1):
+            nc.vector.quantize_mx(
+                out=w_codes[:, c0:c1].bitcast(FP8X4), scales=w_scales[:, c0:c1], in_=woven.rearrange("p m t -> p (m t)")
             )
 
-        w_codes = keep.tile([P, N], U32, name="w_codes", tag="x_then_woven", align_bytes=64)
-        quant_w(woven_early[:], 0, hw)
-        chunks = S // CH
-        first = [psum.tile([P, 2, CH], F32, name="first%d" % u, tag="first%d" % u) for u in range(2)]
-        scores = {c: psum.tile([P, PACK, CH], F32, name="scores%d" % c, tag="scores%d" % c) for c in (1, 3)}
-        third = {1: psum.tile([P, 2, CH], F32, name="third1", tag="third1")}
-        pair = [psum.tile([P, 2, 2 * CH], F32, name="pair0")]
-        very_first = psum.tile([P, CH], F32, name="very_first", tag="whole")
-        whole = []
-        last = []
-
-        def slot(c, t):
-            if (c, t) == (0, 0):
-                return very_first[:]
-            if c in scores:
-                return scores[c][:, t, :]
-            return (first if c == 0 else third)[t // 2][:, t % 2, :]
-
-        pos = {}
-        z = {}
-        z_codes = [keep.tile([P, CH], U32, name="z_codes%d" % c, align_bytes=64) for c in range(chunks)]
-        z_scales = [keep.tile([P, CH], U8, name="z_scales%d" % c, align_bytes=64) for c in range(chunks)]
+        z_codes = [sb([P, CH], U32, "z_codes%d" % c) for c in range(4)]
+        z_scales = [sb([P, CH], U8, "z_scales%d" % c) for c in range(4)]
         out_v = out.rearrange("(a p) j -> p a j", p=P)
 
-        def score(c, slots):
-            for t in slots:
+        def score(c, t0, t1, tag):
+            scores = bank([P, t1 - t0, CH], "scores_%d_%d" % (c, t0), tag)
+            for t in range(t0, t1):
                 nc.tensor.matmul_mx(
-                    out=slot(c, t),
+                    out=scores[:, t - t0, :],
                     lhsT=d_codes[:, t * P : (t + 1) * P].bitcast(FP8X4),
                     lhsT_scale=planes[:, t * P : (t + 1) * P],
-                    rhs=x_all[:, c * CH : (c + 1) * CH].bitcast(FP8X4),
+                    rhs=x_got[:, c * CH : (c + 1) * CH].bitcast(FP8X4),
                     rhs_scale=planes[:, H + c * CH : H + (c + 1) * CH],
                     start=True,
                     stop=True,
                 )
+            return scores
 
-        def positive_scalar(c, tag):
-            pos[c] = keep.tile([P, CH * PACK], F32, name="pos%d" % c, tag=tag, align_bytes=64)
-            for t in range(PACK):
-                nc.scalar.activation(pos[c][:, t * CH : (t + 1) * CH], slot(c, t), ACT.Relu, scale=root[:, t : t + 1])
+        def relu_scalar(pos, scores, t0, t1):
+            for t in range(t0, t1):
+                nc.scalar.activation(pos[:, t * CH : (t + 1) * CH], scores[:, t - t0, :], ACT.Relu, scale=root[:, t : t + 1])
 
-        def positive_vector(c, tag):
-            pos[c] = keep.tile([P, CH * PACK], F32, name="pos%d" % c, tag=tag, align_bytes=64)
+        def relu_vector_slots(pos, scores, t0, t1):
             nc.vector.scalar_tensor_tensor(
-                pos[c][:].rearrange("p (j t) -> p j t", t=PACK),
-                scores[c][:].rearrange("p t j -> p j t"),
+                pos[:, t0 * CH : t1 * CH].rearrange("p (t j) -> p t j", j=CH),
+                scores[:],
+                0.0,
+                root[:, t0:t1].unsqueeze(2).to_broadcast([P, t1 - t0, CH]),
+                ALU.max,
+                ALU.mult,
+            )
+
+        def relu_vector_woven(pos, scores):
+            nc.vector.scalar_tensor_tensor(
+                pos[:].rearrange("p (j t) -> p j t", t=PACK),
+                scores[:].rearrange("p t j -> p j t"),
                 0.0,
                 root[:].unsqueeze(1).to_broadcast([P, CH, PACK]),
                 ALU.max,
                 ALU.mult,
             )
 
-        def positive_shared(c, tag):
-            pos[c] = keep.tile([P, CH * PACK], F32, name="pos%d" % c, tag=tag, align_bytes=64)
-            nc.vector.scalar_tensor_tensor(
-                pos[c][:, 2 * CH : 4 * CH].rearrange("p (t j) -> p t j", t=2),
-                third[1][:],
-                0.0,
-                root[:, 2:4].unsqueeze(2).to_broadcast([P, 2, CH]),
-                ALU.max,
-                ALU.mult,
-            )
-            for t in range(2):
-                nc.scalar.activation(pos[c][:, t * CH : (t + 1) * CH], slot(c, t), ACT.Relu, scale=root[:, t : t + 1])
-
-        def square(c, weaves, tag):
-            z[c] = keep.tile([P, CH * PACK], BF16, name="z%d" % c, tag=tag, align_bytes=64)
+        def square(z, pos, weaves):
             if weaves:
                 nc.scalar.activation(
-                    z[c][:].rearrange("p (c i t) -> p c t i", i=4, t=PACK),
-                    pos[c][:].rearrange("p (t c i) -> p c t i", i=4, t=PACK),
+                    z[:].rearrange("p (c i t) -> p c t i", i=4, t=PACK),
+                    pos[:].rearrange("p (t c i) -> p c t i", i=4, t=PACK),
                     ACT.Square,
                 )
             else:
-                nc.scalar.activation(z[c][:], pos[c][:], ACT.Square)
+                nc.scalar.activation(z[:], pos[:], ACT.Square)
 
-        def quant(c):
-            nc.vector.quantize_mx(out=z_codes[c][:].bitcast(FP8X4), scales=z_scales[c][:], in_=z[c][:])
+        def quant_z(c, z):
+            nc.vector.quantize_mx(out=z_codes[c][:].bitcast(FP8X4), scales=z_scales[c][:], in_=z[:])
 
-        def value(c, blocks):
-            for a in blocks:
-                if c < 2:
-                    dst = pair[a // 2][:, a % 2, c * CH : (c + 1) * CH]
-                elif c == 2:
-                    dst = whole[0][:, a, :]
-                else:
-                    dst = last[a // 2][:, a % 2, :]
-                nc.tensor.matmul_mx(
-                    out=dst,
-                    lhsT=w_codes[:, a * P : (a + 1) * P].bitcast(FP8X4),
-                    lhsT_scale=w_scales[:, a * P : (a + 1) * P],
-                    rhs=z_codes[c][:].bitcast(FP8X4),
-                    rhs_scale=z_scales[c][:],
-                    start=True,
-                    stop=True,
-                )
-
-        def finish(sums, a0, a1, j0, j1, queue, tag):
-            res = keep.tile([P, a1 - a0, j1 - j0], F32, name="res_%d_%d" % (a0, j0), tag=tag, align_bytes=64)
-            nc.vector.tensor_tensor(
-                res[:], sums, cnt_t[:, j0:j1].unsqueeze(1).to_broadcast([P, a1 - a0, j1 - j0]), ALU.mult
-            )
-            queue.dma_start(out_v[:, a0:a1, j0:j1], res[:])
-
-        def weave_late(engine_copy, c0, c1):
-            engine_copy(
-                woven_late[:, c0:c1, :].rearrange("p (c i) t -> p c t i", i=4),
-                cast_late[:, :, c0:c1].rearrange("p t (c i) -> p c t i", i=4),
-            )
-
-        for h in range(2):
+        def value(sums, c, a):
             nc.tensor.matmul_mx(
-                out=scores[2 * h + 1][:].rearrange("p a j -> p (a j)"),
-                lhsT=d_got[:, 0:P].bitcast(FP8X4),
-                lhsT_scale=ds_got[:, 0:P],
-                rhs=d_got[:].bitcast(FP8X4),
-                rhs_scale=ds_got[:],
+                out=sums,
+                lhsT=w_codes[:, a * P : (a + 1) * P].bitcast(FP8X4),
+                lhsT_scale=w_scales[:, a * P : (a + 1) * P],
+                rhs=z_codes[c][:].bitcast(FP8X4),
+                rhs_scale=z_scales[c][:],
                 start=True,
                 stop=True,
             )
-        cnt_t = keep.tile([P, S], F32, name="cnt_t", tag="got_then_cnt", align_bytes=64)
-        nc.sync.dma_start(cnt_t[:], cnt)
-        for c in range(chunks):
-            score(c, (2, 3) if c == 2 else range(PACK))
-        positive_scalar(0, "pos0")
-        third[0] = psum.tile([P, 2, CH], F32, name="third0", tag="first1")
-        score(2, (0, 1))
-        positive_vector(1, "pos1")
-        square(0, True, "z0")
-        square(1, False, "z1")
-        positive_shared(2, "pos2")
-        quant(0)
-        value(0, (0, 1))
-        woven_late = keep.tile([P, hw, PACK], BF16, name="woven_late", tag="pos0", align_bytes=64)
-        weave_late(nc.vector.tensor_copy, 0, hw)
-        quant(1)
-        value(1, (0, 1))
-        quant_w(woven_late[:], hw, N)
-        pair.append(psum.tile([P, 2, 2 * CH], F32, name="pair1", tag="third1"))
-        value(0, (2, 3))
-        value(1, (2, 3))
-        square(2, True, "z2")
-        positive_scalar(3, "z0")
-        finish(pair[0][:], 0, 2, 0, 2 * CH, nc.sync, "r0")
-        quant(2)
-        whole.append(psum.tile([P, N // P, CH], F32, name="whole", tag="whole"))
-        value(2, range(4))
-        square(3, True, "z3")
-        finish(pair[1][:], 2, 4, 0, 2 * CH, nc.sync, "r1")
-        quant(3)
-        last.extend(psum.tile([P, 2, CH], F32, name="last%d" % u, tag="first%d" % u) for u in range(2))
-        value(3, range(4))
-        finish(whole[0][:], 0, 4, 2 * CH, 3 * CH, nc.scalar, "z0")
-        finish(last[0][:], 0, 2, 3 * CH, 4 * CH, nc.sync, "r3")
-        finish(last[1][:], 2, 4, 3 * CH, 4 * CH, nc.scalar, "r4")
+
+        def finish(sums, a0, a1, j0, j1, queue, tag=None):
+            res = sb([P, a1 - a0, j1 - j0], F32, "res_%d_%d" % (a0, j0), tag)
+            nc.vector.tensor_tensor(
+                res[:], sums[:], cnt_t[:, j0:j1].unsqueeze(1).to_broadcast([P, a1 - a0, j1 - j0]), ALU.mult
+            )
+            queue.dma_start(out_v[:, a0:a1, j0:j1], res[:])
+
+        pos = [sb([P, PACK * CH], F32, "pos%d" % c) for c in range(4)]
+        z = [sb([P, PACK * CH], BF16, "z%d" % c) for c in range(4)]
+        quant_w(woven_early[:], 0, HALF)
+        first = [score(0, 0, 1, "b0"), score(0, 1, 2, "b1"), score(0, 2, 4, "b2")]
+        second = score(1, 0, 4, "b3")
+        third_v = score(2, 2, 4, "b4")
+        fourth = score(3, 0, 4, "b5")
+        relu_scalar(pos[0], first[0], 0, 1)
+        relu_scalar(pos[0], first[1], 1, 2)
+        relu_scalar(pos[0], first[2], 2, 4)
+        third_s = score(2, 0, 2, "b2")
+        relu_vector_woven(pos[1], second)
+        square(z[0], pos[0], True)
+        relu_vector_slots(pos[2], third_v, 2, 4)
+        relu_scalar(pos[2], third_s, 0, 2)
+        square(z[1], pos[1], False)
+        quant_z(0, z[0])
+        relu_vector_woven(pos[3], fourth)
+        pair0 = bank([P, 2, 2 * CH], "pair0", "b6")
+        for a in range(2):
+            value(pair0[:, a, 0:CH], 0, a)
+        square(z[2], pos[2], True)
+        square(z[3], pos[3], False)
+        quant_z(1, z[1])
+        for a in range(2):
+            value(pair0[:, a, CH : 2 * CH], 1, a)
+        woven_late = sb([P, HALF, PACK], BF16, "woven_late", "pos0")
+        weave(nc.vector.tensor_copy, woven_late[:], cast_late[:])
+        quant_z(2, z[2])
+        quant_w(woven_late[:], HALF, N)
+        finish(pair0, 0, 2, 0, 2 * CH, nc.sync)
+        pair1 = bank([P, 2, 2 * CH], "pair1", "b7")
+        for c in range(2):
+            for a in range(2):
+                value(pair1[:, a, c * CH : (c + 1) * CH], c, 2 + a)
+        whole = bank([P, 4, CH], "whole", "b0")
+        for a in range(4):
+            value(whole[:, a, :], 2, a)
+        quant_z(3, z[3])
+        finish(pair1, 2, 4, 0, 2 * CH, nc.sync)
+        last = [bank([P, 2, CH], "last%d" % u, tag) for u, tag in enumerate(("b1", "b3"))]
+        for a in range(4):
+            value(last[a // 2][:, a % 2, :], 3, a)
+        finish(whole, 0, 4, 2 * CH, 3 * CH, nc.scalar)
+        finish(last[0], 0, 2, 3 * CH, 4 * CH, nc.sync)
+        finish(last[1], 2, 4, 3 * CH, 4 * CH, nc.scalar)

@@ -39,22 +39,22 @@ def tile_picked_reluattn_relu_p_kernel(tc, x_words, x_scales, d_words, d_scales,
         d_win = sb([P, G], I32, "d_win")
         x_win = sb([P, T], I32, "x_win", "x_then_w")
         gn_t = sb([P, PACK], F32, "gn_t")
-        w_early = [sb([P, n, HALF], F32, "w_early%d" % n) for n in (3, 1)]
+        w_early = [sb([P, 2, HALF], F32, "w_early%d" % u) for u in range(2)]
 
         nc.vector.memset(ds_win[:].bitcast(I32), 0)
         nc.vector.memset(xs_win[:].bitcast(I32), 0)
         w_rows = w1.rearrange("(p t) m -> p t m", t=PACK)
         nc.sync.dma_start(gn_t[:], gn.rearrange("(p t) o -> p (t o)", t=PACK))
-        nc.scalar.dma_start(w_early[0][:], w_rows[:, 0:3, 0:HALF])
+        nc.scalar.dma_start(w_early[0][:], w_rows[:, 0:2, 0:HALF])
         nc.sync.dma_start(kidx_t[:], kidx)
         nc.sync.dma_start(offs_t[:], offs)
         nc.sync.dma_start(ds_win[0:P:8, :].bitcast(I32), d_scales[0].bitcast(I32))
-        nc.sync.dma_start(w_early[1][:], w_rows[:, 3:4, 0:HALF])
+        nc.sync.dma_start(w_early[1][:], w_rows[:, 2:4, 0:HALF])
         nc.sync.dma_start(xs_win[0:P:8, :].bitcast(I32), x_scales[0].bitcast(I32))
         nc.sync.dma_start(d_win[:], d_words[0].rearrange("p n t -> p (n t)").bitcast(I32))
         nc.sync.dma_start(x_win[:], x_words[0].rearrange("p n t -> p (n t)").bitcast(I32))
-        w_late = [sb([P, 2, HALF], F32, "w_late0")]
-        nc.sync.dma_start(w_late[0][:], w_rows[:, 0:2, HALF:N])
+        w_late = [sb([P, 1, HALF], F32, "w_late0")]
+        nc.sync.dma_start(w_late[0][:], w_rows[:, 0:1, HALF:N])
 
         sign = sb([P, PACK], F32, "sign")
         mag = sb([P, PACK], F32, "mag")
@@ -72,12 +72,12 @@ def tile_picked_reluattn_relu_p_kernel(tc, x_words, x_scales, d_words, d_scales,
         cast_early = sb([P, PACK, HALF], BF16, "cast_early")
         woven_early = sb([P, HALF, PACK], BF16, "woven_early")
         for t in range(PACK):
-            nc.scalar.activation(cast_early[:, t, :], w_early[t // 3][:, t % 3, :], ACT.Copy, scale=sign[:, t : t + 1])
+            nc.scalar.activation(cast_early[:, t, :], w_early[t // 2][:, t % 2, :], ACT.Copy, scale=sign[:, t : t + 1])
         weave(nc.scalar.copy, woven_early[:], cast_early[:])
 
         ds_got = sb([P, H], U8, "ds_got")
         xs_got = sb([P, S], U8, "xs_got", "xs_then_w")
-        planes = sb([P, H + S], U8, "planes", "w_early3")
+        planes = sb([P, H + S], U8, "planes", "w_early1")
         nc.vector.tensor_copy(ds_got[:], ds_win[:].indirect(kidx_t[:]))
         nc.vector.tensor_copy(xs_got[:], xs_win[:].indirect(offs_t[:]))
         nc.vector.tensor_copy(
@@ -87,11 +87,11 @@ def tile_picked_reluattn_relu_p_kernel(tc, x_words, x_scales, d_words, d_scales,
         nc.vector.tensor_copy(planes[:, H : H + S].bitcast(I32), xs_got[:].bitcast(I32))
         for r in range(1, 4):
             nc.sync.dma_start(planes[r:P:32, :].bitcast(I32), planes[8 * r : P : 32, :].bitcast(I32))
-        w_late.append(sb([P, 2, HALF], F32, "w_late1", "xs_then_w"))
-        nc.sync.dma_start(w_late[1][:], w_rows[:, 2:4, HALF:N])
+        w_late.append(sb([P, 3, HALF], F32, "w_late1", "xs_then_w"))
+        nc.sync.dma_start(w_late[1][:], w_rows[:, 1:4, HALF:N])
         cast_late = sb([P, PACK, HALF], BF16, "cast_late")
         for t in range(PACK):
-            nc.gpsimd.tensor_scalar(cast_late[:, t, :], w_late[t // 2][:, t % 2, :], sign[:, t : t + 1], 0.0, ALU.mult, ALU.add)
+            nc.gpsimd.tensor_scalar(cast_late[:, t, :], w_late[min(t, 1)][:, max(t - 1, 0), :], sign[:, t : t + 1], 0.0, ALU.mult, ALU.add)
 
         d_got = sb([P, H], U32, "d_got", "got_then_cnt")
         d_codes = sb([P, H], U32, "d_codes")
@@ -192,7 +192,7 @@ def tile_picked_reluattn_relu_p_kernel(tc, x_words, x_scales, d_words, d_scales,
             )
             queue.dma_start(out_v[:, a0:a1, j0:j1], res[:])
 
-        pos = [sb([P, PACK * CH], F32, "pos%d" % c) for c in range(4)]
+        pos = [sb([P, PACK * CH], F32, "pos%d" % c) for c in range(3)]
         z = [sb([P, PACK * CH], BF16, "z%d" % c) for c in range(4)]
         quant_w(woven_early[:], 0, HALF)
         first = [score(0, 0, 1, "b0"), score(0, 1, 2, "b1"), score(0, 2, 4, "b2")]
@@ -205,36 +205,34 @@ def tile_picked_reluattn_relu_p_kernel(tc, x_words, x_scales, d_words, d_scales,
         third_s = score(2, 0, 2, "b2")
         relu_vector_woven(pos[1], second)
         square(z[0], pos[0], True)
+        square(z[1], pos[1], False)
         relu_vector_slots(pos[2], third_v, 2, 4)
         relu_scalar(pos[2], third_s, 0, 2)
-        square(z[1], pos[1], False)
+
+        def values(chunks, a0, a1, tag):
+            sums = bank([P, a1 - a0, len(chunks) * CH], "sums_%d_%d" % (chunks[0], a0), tag)
+            for u, c in enumerate(chunks):
+                for a in range(a0, a1):
+                    value(sums[:, a - a0, u * CH : (u + 1) * CH], c, a)
+            return sums
+
         quant_z(0, z[0])
-        relu_vector_woven(pos[3], fourth)
-        pair0 = bank([P, 2, 2 * CH], "pair0", "b6")
-        for a in range(2):
-            value(pair0[:, a, 0:CH], 0, a)
-        square(z[2], pos[2], True)
-        square(z[3], pos[3], False)
-        quant_z(1, z[1])
-        for a in range(2):
-            value(pair0[:, a, CH : 2 * CH], 1, a)
         woven_late = sb([P, HALF, PACK], BF16, "woven_late", "pos0")
         weave(nc.vector.tensor_copy, woven_late[:], cast_late[:])
-        quant_z(2, z[2])
+        quant_z(1, z[1])
+        front = values((0, 1), 0, 2, "b6")
         quant_w(woven_late[:], HALF, N)
-        finish(pair0, 0, 2, 0, 2 * CH, nc.sync)
-        pair1 = bank([P, 2, 2 * CH], "pair1", "b7")
-        for c in range(2):
-            for a in range(2):
-                value(pair1[:, a, c * CH : (c + 1) * CH], c, 2 + a)
-        whole = bank([P, 4, CH], "whole", "b0")
-        for a in range(4):
-            value(whole[:, a, :], 2, a)
+        back = values((0, 1), 2, 4, "b4")
+        square(z[2], pos[2], True)
+        pos.append(sb([P, PACK * CH], F32, "pos3", "z0"))
+        relu_scalar(pos[3], fourth, 0, 4)
+        finish(front, 0, 2, 0, 2 * CH, nc.sync)
+        quant_z(2, z[2])
+        whole = values((2,), 0, 4, "b0")
+        square(z[3], pos[3], True)
+        finish(back, 2, 4, 0, 2 * CH, nc.sync)
         quant_z(3, z[3])
-        finish(pair1, 2, 4, 0, 2 * CH, nc.sync)
-        last = [bank([P, 2, CH], "last%d" % u, tag) for u, tag in enumerate(("b1", "b3"))]
-        for a in range(4):
-            value(last[a // 2][:, a % 2, :], 3, a)
-        finish(whole, 0, 4, 2 * CH, 3 * CH, nc.scalar)
+        last = [values((3,), 0, 2, "b1"), values((3,), 2, 4, "b2")]
+        finish(whole, 0, 4, 2 * CH, 3 * CH, nc.scalar, "z0")
         finish(last[0], 0, 2, 3 * CH, 4 * CH, nc.sync)
         finish(last[1], 2, 4, 3 * CH, 4 * CH, nc.scalar)

@@ -89,9 +89,9 @@ def tile_picked_reluattn_relu_p_kernel(tc, x_words, x_scales, d_words, d_scales,
             nc.sync.dma_start(planes[r:P:32, :].bitcast(I32), planes[8 * r : P : 32, :].bitcast(I32))
         w_late.append(sb([P, 3, HALF], F32, "w_late1", "xs_then_w"))
         nc.sync.dma_start(w_late[1][:], w_rows[:, 1:4, HALF:N])
-        cast_late = sb([P, PACK, HALF], BF16, "cast_late")
+        cast_late = sb([P, 2, HALF, 2], BF16, "cast_late")
         for t in range(PACK):
-            nc.gpsimd.tensor_scalar(cast_late[:, t, :], w_late[min(t, 1)][:, max(t - 1, 0), :], sign[:, t : t + 1], 0.0, ALU.mult, ALU.add)
+            nc.gpsimd.tensor_scalar(cast_late[:, t // 2, :, t % 2], w_late[min(t, 1)][:, max(t - 1, 0), :], sign[:, t : t + 1], 0.0, ALU.mult, ALU.add)
 
         d_got = sb([P, H], U32, "d_got", "got_then_cnt")
         d_codes = sb([P, H], U32, "d_codes")
@@ -151,25 +151,12 @@ def tile_picked_reluattn_relu_p_kernel(tc, x_words, x_scales, d_words, d_scales,
                 ALU.mult,
             )
 
-        def relu_vector_woven(pos, scores):
-            nc.vector.scalar_tensor_tensor(
-                pos[:].rearrange("p (j t) -> p j t", t=PACK),
-                scores[:].rearrange("p t j -> p j t"),
-                0.0,
-                root[:].unsqueeze(1).to_broadcast([P, CH, PACK]),
-                ALU.max,
-                ALU.mult,
+        def square(z, pos):
+            nc.scalar.activation(
+                z[:].rearrange("p (c i t) -> p c t i", i=4, t=PACK),
+                pos[:].rearrange("p (t c i) -> p c t i", i=4, t=PACK),
+                ACT.Square,
             )
-
-        def square(z, pos, weaves):
-            if weaves:
-                nc.scalar.activation(
-                    z[:].rearrange("p (c i t) -> p c t i", i=4, t=PACK),
-                    pos[:].rearrange("p (t c i) -> p c t i", i=4, t=PACK),
-                    ACT.Square,
-                )
-            else:
-                nc.scalar.activation(z[:], pos[:], ACT.Square)
 
         def quant_z(c, z):
             nc.vector.quantize_mx(out=z_codes[c][:].bitcast(FP8X4), scales=z_scales[c][:], in_=z[:])
@@ -196,18 +183,17 @@ def tile_picked_reluattn_relu_p_kernel(tc, x_words, x_scales, d_words, d_scales,
         z = [sb([P, PACK * CH], BF16, "z%d" % c) for c in range(4)]
         quant_w(woven_early[:], 0, HALF)
         first = [score(0, 0, 1, "b0"), score(0, 1, 2, "b1"), score(0, 2, 4, "b2")]
-        second = score(1, 0, 4, "b3")
-        third_v = score(2, 2, 4, "b4")
+        second = [score(1, 0, 2, "b3"), score(1, 2, 4, "b7")]
+        third = score(2, 0, 4, "b4")
         fourth = score(3, 0, 4, "b5")
         relu_scalar(pos[0], first[0], 0, 1)
         relu_scalar(pos[0], first[1], 1, 2)
         relu_scalar(pos[0], first[2], 2, 4)
-        third_s = score(2, 0, 2, "b2")
-        relu_vector_woven(pos[1], second)
-        square(z[0], pos[0], True)
-        square(z[1], pos[1], False)
-        relu_vector_slots(pos[2], third_v, 2, 4)
-        relu_scalar(pos[2], third_s, 0, 2)
+        relu_vector_slots(pos[1], second[0], 0, 2)
+        relu_vector_slots(pos[1], second[1], 2, 4)
+        square(z[0], pos[0])
+        square(z[1], pos[1])
+        relu_vector_slots(pos[2], third, 0, 4)
 
         def values(chunks, a0, a1, tag):
             sums = bank([P, a1 - a0, len(chunks) * CH], "sums_%d_%d" % (chunks[0], a0), tag)
@@ -218,18 +204,21 @@ def tile_picked_reluattn_relu_p_kernel(tc, x_words, x_scales, d_words, d_scales,
 
         quant_z(0, z[0])
         woven_late = sb([P, HALF, PACK], BF16, "woven_late", "pos0")
-        weave(nc.vector.tensor_copy, woven_late[:], cast_late[:])
+        nc.vector.tensor_copy(
+            woven_late[:].rearrange("p m t -> p (m t)").bitcast(F32).rearrange("p (m u) -> p m u", u=2),
+            cast_late[:].rearrange("p u m e -> p (u m e)").bitcast(F32).rearrange("p (u m) -> p m u", u=2),
+        )
         quant_z(1, z[1])
         front = values((0, 1), 0, 2, "b6")
         quant_w(woven_late[:], HALF, N)
         back = values((0, 1), 2, 4, "b4")
-        square(z[2], pos[2], True)
+        square(z[2], pos[2])
         pos.append(sb([P, PACK * CH], F32, "pos3", "z0"))
         relu_scalar(pos[3], fourth, 0, 4)
         finish(front, 0, 2, 0, 2 * CH, nc.sync)
         quant_z(2, z[2])
         whole = values((2,), 0, 4, "b0")
-        square(z[3], pos[3], True)
+        square(z[3], pos[3])
         finish(back, 2, 4, 0, 2 * CH, nc.sync)
         quant_z(3, z[3])
         last = [values((3,), 0, 2, "b1"), values((3,), 2, 4, "b2")]

@@ -37,7 +37,7 @@ def tile_picked_reluattn_relu_p_kernel(tc, x_words, x_scales, d_words, d_scales,
         ds_win = sb([P, G], U8, "ds_win")
         xs_win = sb([P, T], U8, "xs_win")
         d_win = sb([P, G], I32, "d_win")
-        x_win = sb([P, T], I32, "x_win", "x_then_w")
+        x_win = sb([P, T], I32, "x_win")
         gn_t = sb([P, PACK], F32, "gn_t")
         w_early = [sb([P, 2, HALF], F32, "w_early%d" % u) for u in range(2)]
 
@@ -88,10 +88,11 @@ def tile_picked_reluattn_relu_p_kernel(tc, x_words, x_scales, d_words, d_scales,
         for r in range(1, 4):
             nc.sync.dma_start(planes[r:P:32, :].bitcast(I32), planes[8 * r : P : 32, :].bitcast(I32))
         w_late.append(sb([P, 3, HALF], F32, "w_late1", "xs_then_w"))
-        nc.sync.dma_start(w_late[1][:], w_rows[:, 1:4, HALF:N])
+        nc.sync.dma_start(w_late[1][:, 0:1, :], w_rows[:, 1:2, HALF:N])
+        nc.sync.dma_start(w_late[1][:, 1:3, :], w_rows[:, 2:4, HALF:N])
         cast_late = sb([P, 2, HALF, 2], BF16, "cast_late")
-        for t in range(PACK):
-            nc.gpsimd.tensor_scalar(cast_late[:, t // 2, :, t % 2], w_late[min(t, 1)][:, max(t - 1, 0), :], sign[:, t : t + 1], 0.0, ALU.mult, ALU.add)
+        for t in range(2, PACK):
+            nc.gpsimd.tensor_scalar(cast_late[:, 1, :, t - 2], w_late[1][:, t - 1, :], sign[:, t : t + 1], 0.0, ALU.mult, ALU.add)
 
         d_got = sb([P, H], U32, "d_got", "got_then_cnt")
         d_codes = sb([P, H], U32, "d_codes")
@@ -111,7 +112,10 @@ def tile_picked_reluattn_relu_p_kernel(tc, x_words, x_scales, d_words, d_scales,
         for j0, j1 in ((0, 128), (128, 256), (256, 512)):
             nc.vector.tensor_copy(x_got[:, j0:j1], x_win[:].bitcast(U32).indirect(offs_t[:, j0 // 16 : j1 // 16]))
 
-        w_codes = sb([P, N], U32, "w_codes", "x_then_w")
+        for t in range(2):
+            nc.vector.tensor_scalar(cast_late[:, 0, :, t], w_late[t][:, 0, :], sign[:, t : t + 1], None, ALU.mult)
+
+        w_codes = sb([P, N], U32, "w_codes")
         w_scales = sb([P, N], U8, "w_scales")
 
         def quant_w(woven, c0, c1):

@@ -188,16 +188,17 @@ def tile_picked_reluattn_relu_p_kernel(tc, x_words, x_scales, d_words, d_scales,
         quant_w(woven_early[:], 0, HALF)
         first = [score(0, 0, 1, "b0"), score(0, 1, 2, "b1"), score(0, 2, 4, "b2")]
         second = [score(1, 0, 2, "b3"), score(1, 2, 4, "b7")]
-        third = score(2, 0, 4, "b4")
-        fourth = score(3, 0, 4, "b5")
         relu_scalar(pos[0], first[0], 0, 1)
+        third = [score(2, 0, 2, "b4"), score(2, 2, 4, "b0")]
+        fourth = score(3, 0, 4, "b5")
         relu_scalar(pos[0], first[1], 1, 2)
         relu_scalar(pos[0], first[2], 2, 4)
         relu_vector_slots(pos[1], second[0], 0, 2)
         relu_vector_slots(pos[1], second[1], 2, 4)
         square(z[0], pos[0])
         square(z[1], pos[1])
-        relu_vector_slots(pos[2], third, 0, 4)
+        relu_vector_slots(pos[2], third[0], 0, 2)
+        relu_vector_slots(pos[2], third[1], 2, 4)
 
         def values(chunks, a0, a1, tag):
             sums = bank([P, a1 - a0, len(chunks) * CH], "sums_%d_%d" % (chunks[0], a0), tag)
@@ -217,15 +218,15 @@ def tile_picked_reluattn_relu_p_kernel(tc, x_words, x_scales, d_words, d_scales,
         quant_w(woven_late[:], HALF, N)
         back = values((0, 1), 2, 4, "b4")
         square(z[2], pos[2])
-        pos.append(sb([P, PACK * CH], F32, "pos3", "z0"))
+        pos.append(sb([P, PACK * CH], F32, "pos3", "pos1"))
         relu_scalar(pos[3], fourth, 0, 4)
-        finish(front, 0, 2, 0, 2 * CH, nc.sync)
         quant_z(2, z[2])
         whole = values((2,), 0, 4, "b0")
+        finish(front, 0, 2, 0, 2 * CH, nc.sync)
         square(z[3], pos[3])
         finish(back, 2, 4, 0, 2 * CH, nc.sync)
         quant_z(3, z[3])
         last = [values((3,), 0, 2, "b1"), values((3,), 2, 4, "b2")]
-        finish(whole, 0, 4, 2 * CH, 3 * CH, nc.scalar, "z0")
+        finish(whole, 0, 4, 2 * CH, 3 * CH, nc.scalar, "pos1")
         finish(last[0], 0, 2, 3 * CH, 4 * CH, nc.sync)
         finish(last[1], 2, 4, 3 * CH, 4 * CH, nc.scalar)

@@ -53,8 +53,8 @@ def tile_picked_reluattn_relu_p_kernel(tc, x_words, x_scales, d_words, d_scales,
         nc.sync.dma_start(xs_win[0:P:8, :].bitcast(I32), x_scales[0].bitcast(I32))
         nc.sync.dma_start(d_win[:], d_words[0].rearrange("p n t -> p (n t)").bitcast(I32))
         nc.sync.dma_start(x_win[:], x_words[0].rearrange("p n t -> p (n t)").bitcast(I32))
-        w_late = [sb([P, 1, HALF], F32, "w_late0")]
-        nc.sync.dma_start(w_late[0][:], w_rows[:, 0:1, HALF:N])
+        w_late = [sb([P, 2, HALF], F32, "w_late0")]
+        nc.sync.dma_start(w_late[0][:], w_rows[:, 0:2, HALF:N])
 
         sign = sb([P, PACK], F32, "sign")
         mag = sb([P, PACK], F32, "mag")
@@ -87,12 +87,11 @@ def tile_picked_reluattn_relu_p_kernel(tc, x_words, x_scales, d_words, d_scales,
         nc.vector.tensor_copy(planes[:, H : H + S].bitcast(I32), xs_got[:].bitcast(I32))
         for r in range(1, 4):
             nc.sync.dma_start(planes[r:P:32, :].bitcast(I32), planes[8 * r : P : 32, :].bitcast(I32))
-        w_late.append(sb([P, 3, HALF], F32, "w_late1", "xs_then_w"))
-        nc.sync.dma_start(w_late[1][:, 0:1, :], w_rows[:, 1:2, HALF:N])
-        nc.sync.dma_start(w_late[1][:, 1:3, :], w_rows[:, 2:4, HALF:N])
+        w_late.append(sb([P, 2, HALF], F32, "w_late1", "xs_then_w"))
+        nc.sync.dma_start(w_late[1][:], w_rows[:, 2:4, HALF:N])
         cast_late = sb([P, 2, HALF, 2], BF16, "cast_late")
         for t in range(2, PACK):
-            nc.gpsimd.tensor_scalar(cast_late[:, 1, :, t - 2], w_late[1][:, t - 1, :], sign[:, t : t + 1], 0.0, ALU.mult, ALU.add)
+            nc.gpsimd.tensor_scalar(cast_late[:, 1, :, t - 2], w_late[1][:, t - 2, :], sign[:, t : t + 1], 0.0, ALU.mult, ALU.add)
 
         d_got = sb([P, H], U32, "d_got", "got_then_cnt")
         d_codes = sb([P, H], U32, "d_codes")
@@ -113,7 +112,7 @@ def tile_picked_reluattn_relu_p_kernel(tc, x_words, x_scales, d_words, d_scales,
             nc.vector.tensor_copy(x_got[:, j0:j1], x_win[:].bitcast(U32).indirect(offs_t[:, j0 // 16 : j1 // 16]))
 
         for t in range(2):
-            nc.vector.tensor_scalar(cast_late[:, 0, :, t], w_late[t][:, 0, :], sign[:, t : t + 1], None, ALU.mult)
+            nc.vector.tensor_scalar(cast_late[:, 0, :, t], w_late[0][:, t, :], sign[:, t : t + 1], None, ALU.mult)
 
         w_codes = sb([P, N], U32, "w_codes")
         w_scales = sb([P, N], U8, "w_scales")

@@ -17,6 +17,8 @@ P = 128
 PACK = 4
 CH = 128
 HALF = N // 2
+WARM_M = 32
+WARM_PASSES = 3
 FLOPS = 2 * K * H * S + 2 * H * N * S
 
 
@@ -43,6 +45,9 @@ def tile_picked_reluattn_relu_p_kernel(tc, x_words, x_scales, d_words, d_scales,
 
         nc.vector.memset(ds_win[:].bitcast(I32), 0)
         nc.vector.memset(xs_win[:].bitcast(I32), 0)
+        w_codes = sb([P, N], U32, "w_codes")
+        w_scales = sb([P, N], U8, "w_scales")
+        nc.vector.memset(w_scales[:].bitcast(I32), 0)
         w_rows = w1.rearrange("(p t) m -> p t m", t=PACK)
         nc.sync.dma_start(gn_t[:], gn.rearrange("(p t) o -> p (t o)", t=PACK))
         nc.scalar.dma_start(w_early[0][:], w_rows[:, 0:2, 0:HALF])
@@ -114,9 +119,6 @@ def tile_picked_reluattn_relu_p_kernel(tc, x_words, x_scales, d_words, d_scales,
         for t in range(2):
             nc.vector.tensor_scalar(cast_late[:, 0, :, t], w_late[0][:, t, :], sign[:, t : t + 1], None, ALU.mult)
 
-        w_codes = sb([P, N], U32, "w_codes")
-        w_scales = sb([P, N], U8, "w_scales")
-
         def quant_w(woven, c0, c1):
             nc.vector.quantize_mx(
                 out=w_codes[:, c0:c1].bitcast(FP8X4), scales=w_scales[:, c0:c1], in_=woven.rearrange("p m t -> p (m t)")
@@ -185,6 +187,19 @@ def tile_picked_reluattn_relu_p_kernel(tc, x_words, x_scales, d_words, d_scales,
         pos = [sb([P, PACK * CH], F32, "pos%d" % c) for c in range(3)]
         z = [sb([P, PACK * CH], BF16, "z%d" % c) for c in range(4)]
         quant_w(woven_early[:], 0, HALF)
+        nc.scalar.copy(w_codes[:, HALF:N], w_codes[:, 0:HALF])
+        nc.scalar.copy(w_scales[:, HALF:N].bitcast(U32), w_scales[:, 0:HALF].bitcast(U32))
+        warm = bank([WARM_M, N], "warm", "b6")
+        for u in range(WARM_PASSES):
+            nc.tensor.matmul_mx(
+                out=warm[:],
+                lhsT=w_codes[:, 0:WARM_M].bitcast(FP8X4),
+                lhsT_scale=w_scales[:, 0:WARM_M],
+                rhs=w_codes[:].bitcast(FP8X4),
+                rhs_scale=w_scales[:],
+                start=True,
+                stop=True,
+            )
         first = [score(0, 0, 1, "b0"), score(0, 1, 2, "b1"), score(0, 2, 4, "b2")]
         second = [score(1, 0, 2, "b3"), score(1, 2, 4, "b7")]
         relu_scalar(pos[0], first[0], 0, 1)

@@ -200,15 +200,17 @@ def tile_picked_reluattn_relu_p_kernel(tc, x_words, x_scales, d_words, d_scales,
                 start=True,
                 stop=True,
             )
-        first = [score(0, 0, 1, "b0"), score(0, 1, 2, "b1"), score(0, 2, 4, "b2")]
-        second = [score(1, 0, 2, "b3"), score(1, 2, 4, "b7")]
-        relu_scalar(pos[0], first[0], 0, 1)
+        first = [score(0, t, t + 1, tag) for t, tag in enumerate(("b0", "b1", "b2", "b6"))]
+        second = [score(1, 0, 2, "b3"), score(1, 3, 4, "b5"), score(1, 2, 3, "b7")]
+        for t in range(2):
+            relu_scalar(pos[0], first[t], t, t + 1)
         third = [score(2, 0, 2, "b4"), score(2, 2, 4, "b0")]
-        fourth = score(3, 0, 4, "b5")
-        relu_scalar(pos[0], first[1], 1, 2)
-        relu_scalar(pos[0], first[2], 2, 4)
+        fourth = score(3, 0, 4, "b1")
+        for t in range(2, PACK):
+            relu_scalar(pos[0], first[t], t, t + 1)
+        relu_scalar(pos[1], second[1], 3, 4)
         relu_vector_slots(pos[1], second[0], 0, 2)
-        relu_vector_slots(pos[1], second[1], 2, 4)
+        relu_vector_slots(pos[1], second[2], 2, 3)
         square(z[0], pos[0])
         square(z[1], pos[1])
         relu_vector_slots(pos[2], third[0], 0, 2)
@@ -224,8 +226,8 @@ def tile_picked_reluattn_relu_p_kernel(tc, x_words, x_scales, d_words, d_scales,
         quant_z(0, z[0])
         woven_late = sb([P, HALF, PACK], BF16, "woven_late", "pos0")
         nc.vector.tensor_copy(
-            woven_late[:].rearrange("p m t -> p (m t)").bitcast(F32).rearrange("p (m u) -> p m u", u=2),
-            cast_late[:].rearrange("p u m e -> p (u m e)").bitcast(F32).rearrange("p (u m) -> p m u", u=2),
+            woven_late[:].rearrange("p m t -> p (m t)").bitcast(F32).rearrange("p (c i u) -> p c u i", i=2, u=2),
+            cast_late[:].rearrange("p u m e -> p (u m e)").bitcast(F32).rearrange("p (u c i) -> p c u i", i=2, u=2),
         )
         quant_z(1, z[1])
         front = values((0, 1), 0, 2, "b6")
@@ -240,7 +242,7 @@ def tile_picked_reluattn_relu_p_kernel(tc, x_words, x_scales, d_words, d_scales,
         square(z[3], pos[3])
         finish(back, 2, 4, 0, 2 * CH, nc.sync)
         quant_z(3, z[3])
-        last = [values((3,), 0, 2, "b1"), values((3,), 2, 4, "b2")]
+        last = [values((3,), 0, 2, "b5"), values((3,), 2, 4, "b2")]
         finish(whole, 0, 4, 2 * CH, 3 * CH, nc.scalar, "pos1")
         finish(last[0], 0, 2, 3 * CH, 4 * CH, nc.sync)
         finish(last[1], 2, 4, 3 * CH, 4 * CH, nc.scalar)

@@ -18,7 +18,7 @@ PACK = 4
 CH = 128
 HALF = N // 2
 WARM_M = 32
-WARM_PASSES = 3
+WARM_WIDTHS = (P, P, P, N, N)
 FLOPS = 2 * K * H * S + 2 * H * N * S
 
 
@@ -190,13 +190,13 @@ def tile_picked_reluattn_relu_p_kernel(tc, x_words, x_scales, d_words, d_scales,
         nc.scalar.copy(w_codes[:, HALF:N], w_codes[:, 0:HALF])
         nc.scalar.copy(w_scales[:, HALF:N].bitcast(U32), w_scales[:, 0:HALF].bitcast(U32))
         warm = bank([WARM_M, N], "warm", "b6")
-        for u in range(WARM_PASSES):
+        for width in WARM_WIDTHS:
             nc.tensor.matmul_mx(
-                out=warm[:],
+                out=warm[:, 0:width],
                 lhsT=w_codes[:, 0:WARM_M].bitcast(FP8X4),
                 lhsT_scale=w_scales[:, 0:WARM_M],
-                rhs=w_codes[:].bitcast(FP8X4),
-                rhs_scale=w_scales[:],
+                rhs=w_codes[:, 0:width].bitcast(FP8X4),
+                rhs_scale=w_scales[:, 0:width],
                 start=True,
                 stop=True,
             )

from contextlib import ExitStack

import concourse.mybir as mybir

F32 = mybir.dt.float32
BF16 = mybir.dt.bfloat16
I32 = mybir.dt.int32
U32 = mybir.dt.uint32
U16 = mybir.dt.uint16
U8 = mybir.dt.uint8
FP8X4 = mybir.dt.float8_e4m3fn_x4
ALU = mybir.AluOpType
ACT = mybir.ActivationFunctionType

K, T, S, N, G, H = 512, 2048, 512, 512, 2048, 512
P = 128
PACK = 4
CH = 128
HALF = N // 2
WARM_M = 32
WARM_WIDTHS = (P, P, P, N, N)
FLOPS = 2 * K * H * S + 2 * H * N * S


def tile_picked_reluattn_relu_p_kernel(tc, x_words, x_scales, d_words, d_scales, cnt, gn, w1, offs, kidx, out):
    nc = tc.nc
    with ExitStack() as ctx:
        keep = ctx.enter_context(tc.tile_pool(name="keep", bufs=1))
        psum = ctx.enter_context(tc.psum_pool(name="psum", bufs=1))

        def sb(shape, dtype, name, tag=None):
            return keep.tile(shape, dtype, name=name, tag=tag or name, align_bytes=64)

        def bank(shape, name, tag):
            return psum.tile(shape, F32, name=name, tag=tag)

        kidx_t = keep.tile([P, H // 16], U16, name="kidx_t")
        offs_t = keep.tile([P, S // 16], U16, name="offs_t")
        ds_win = sb([P, G], U8, "ds_win")
        xs_win = sb([P, T], U8, "xs_win")
        d_win = sb([P, G], I32, "d_win")
        x_win = sb([P, T], I32, "x_win")
        gn_t = sb([P, PACK], F32, "gn_t")
        w_early = [sb([P, 2, HALF], F32, "w_early%d" % u) for u in range(2)]

        nc.vector.memset(ds_win[:].bitcast(I32), 0)
        nc.vector.memset(xs_win[:].bitcast(I32), 0)
        w_codes = sb([P, N], U32, "w_codes")
        w_scales = sb([P, N], U8, "w_scales")
        nc.vector.memset(w_scales[:].bitcast(I32), 0)
        w_rows = w1.rearrange("(p t) m -> p t m", t=PACK)
        nc.sync.dma_start(gn_t[:], gn.rearrange("(p t) o -> p (t o)", t=PACK))
        nc.scalar.dma_start(w_early[0][:], w_rows[:, 0:2, 0:HALF])
        nc.sync.dma_start(kidx_t[:], kidx)
        nc.sync.dma_start(offs_t[:], offs)
        nc.sync.dma_start(ds_win[0:P:8, :].bitcast(I32), d_scales[0].bitcast(I32))
        nc.sync.dma_start(w_early[1][:], w_rows[:, 2:4, 0:HALF])
        nc.sync.dma_start(xs_win[0:P:8, :].bitcast(I32), x_scales[0].bitcast(I32))
        nc.sync.dma_start(d_win[:], d_words[0].rearrange("p n t -> p (n t)").bitcast(I32))
        nc.sync.dma_start(x_win[:], x_words[0].rearrange("p n t -> p (n t)").bitcast(I32))
        w_late = [sb([P, 2, HALF], F32, "w_late0")]
        nc.sync.dma_start(w_late[0][:], w_rows[:, 0:2, HALF:N])

        sign = sb([P, PACK], F32, "sign")
        mag = sb([P, PACK], F32, "mag")
        root = sb([P, PACK], F32, "root")
        nc.vector.scalar_tensor_tensor(mag[:], gn_t[:], -1.0, gn_t[:], ALU.mult, ALU.max)
        nc.vector.tensor_scalar(sign[:], gn_t[:], 0.0, 0.5, ALU.is_ge, ALU.subtract)
        nc.scalar.activation(root[:], mag[:], ACT.Sqrt, scale=2.0 * 0.0625 * 0.0625)

        def weave(copy, woven, cast):
            copy(
                woven.rearrange("p (c i) t -> p c t i", i=4),
                cast.rearrange("p t (c i) -> p c t i", i=4),
            )

        cast_early = sb([P, PACK, HALF], BF16, "cast_early")
        woven_early = sb([P, HALF, PACK], BF16, "woven_early")
        for t in range(PACK):
            nc.scalar.activation(cast_early[:, t, :], w_early[t // 2][:, t % 2, :], ACT.Copy, scale=sign[:, t : t + 1])
        weave(nc.scalar.copy, woven_early[:], cast_early[:])

        ds_got = sb([P, H], U8, "ds_got")
        xs_got = sb([P, S], U8, "xs_got", "xs_then_w")
        planes = sb([P, H + S], U8, "planes", "w_early1")
        nc.vector.tensor_copy(ds_got[:], ds_win[:].indirect(kidx_t[:]))
        nc.vector.tensor_copy(xs_got[:], xs_win[:].indirect(offs_t[:]))
        nc.vector.tensor_copy(
            planes[:, 0:H].rearrange("p (t m) -> p t m", t=PACK),
            ds_got[:].rearrange("p (m t) -> p t m", t=PACK),
        )
        nc.vector.tensor_copy(planes[:, H : H + S].bitcast(I32), xs_got[:].bitcast(I32))
        for r in range(1, 4):
            nc.sync.dma_start(planes[r:P:32, :].bitcast(I32), planes[8 * r : P : 32, :].bitcast(I32))
        w_late.append(sb([P, 2, HALF], F32, "w_late1", "xs_then_w"))
        nc.sync.dma_start(w_late[1][:], w_rows[:, 2:4, HALF:N])
        cast_late = sb([P, 2, HALF, 2], BF16, "cast_late")
        for t in range(2, PACK):
            nc.gpsimd.tensor_scalar(cast_late[:, 1, :, t - 2], w_late[1][:, t - 2, :], sign[:, t : t + 1], 0.0, ALU.mult, ALU.add)

        d_got = sb([P, H], U32, "d_got", "got_then_cnt")
        d_codes = sb([P, H], U32, "d_codes")
        for u in range(2):
            nc.vector.tensor_copy(
                d_got[:, u * 256 : (u + 1) * 256], d_win[:].bitcast(U32).indirect(kidx_t[:, u * 16 : (u + 1) * 16])
            )
        for u in range(2):
            nc.vector.tensor_copy(
                d_codes[:].rearrange("p (t m) -> p m t", t=PACK)[:, u * 64 : (u + 1) * 64, :],
                d_got[:, u * 256 : (u + 1) * 256].rearrange("p (m t) -> p m t", t=PACK),
            )
        cnt_t = sb([P, S], F32, "cnt_t", "got_then_cnt")
        nc.sync.dma_start(cnt_t[:], cnt)

        x_got = sb([P, S], U32, "x_got")
        for j0, j1 in ((0, 128), (128, 256), (256, 512)):
            nc.vector.tensor_copy(x_got[:, j0:j1], x_win[:].bitcast(U32).indirect(offs_t[:, j0 // 16 : j1 // 16]))

        for t in range(2):
            nc.vector.tensor_scalar(cast_late[:, 0, :, t], w_late[0][:, t, :], sign[:, t : t + 1], None, ALU.mult)

        def quant_w(woven, c0, c1):
            nc.vector.quantize_mx(
                out=w_codes[:, c0:c1].bitcast(FP8X4), scales=w_scales[:, c0:c1], in_=woven.rearrange("p m t -> p (m t)")
            )

        z_codes = [sb([P, CH], U32, "z_codes%d" % c) for c in range(4)]
        z_scales = [sb([P, CH], U8, "z_scales%d" % c) for c in range(4)]
        out_v = out.rearrange("(a p) j -> p a j", p=P)

        def score(c, t0, t1, tag):
            scores = bank([P, t1 - t0, CH], "scores_%d_%d" % (c, t0), tag)
            for t in range(t0, t1):
                nc.tensor.matmul_mx(
                    out=scores[:, t - t0, :],
                    lhsT=d_codes[:, t * P : (t + 1) * P].bitcast(FP8X4),
                    lhsT_scale=planes[:, t * P : (t + 1) * P],
                    rhs=x_got[:, c * CH : (c + 1) * CH].bitcast(FP8X4),
                    rhs_scale=planes[:, H + c * CH : H + (c + 1) * CH],
                    start=True,
                    stop=True,
                )
            return scores

        def relu_scalar(pos, scores, t0, t1):
            for t in range(t0, t1):
                nc.scalar.activation(pos[:, t * CH : (t + 1) * CH], scores[:, t - t0, :], ACT.Relu, scale=root[:, t : t + 1])

        def relu_vector_slots(pos, scores, t0, t1):
            nc.vector.scalar_tensor_tensor(
                pos[:, t0 * CH : t1 * CH].rearrange("p (t j) -> p t j", j=CH),
                scores[:],
                0.0,
                root[:, t0:t1].unsqueeze(2).to_broadcast([P, t1 - t0, CH]),
                ALU.max,
                ALU.mult,
            )

        def square(z, pos):
            nc.scalar.activation(
                z[:].rearrange("p (c i t) -> p c t i", i=4, t=PACK),
                pos[:].rearrange("p (t c i) -> p c t i", i=4, t=PACK),
                ACT.Square,
            )

        def quant_z(c, z):
            nc.vector.quantize_mx(out=z_codes[c][:].bitcast(FP8X4), scales=z_scales[c][:], in_=z[:])

        def value(sums, c, a):
            nc.tensor.matmul_mx(
                out=sums,
                lhsT=w_codes[:, a * P : (a + 1) * P].bitcast(FP8X4),
                lhsT_scale=w_scales[:, a * P : (a + 1) * P],
                rhs=z_codes[c][:].bitcast(FP8X4),
                rhs_scale=z_scales[c][:],
                start=True,
                stop=True,
            )

        def finish(sums, a0, a1, j0, j1, queue, tag=None):
            res = sb([P, a1 - a0, j1 - j0], F32, "res_%d_%d" % (a0, j0), tag)
            nc.vector.tensor_tensor(
                res[:], sums[:], cnt_t[:, j0:j1].unsqueeze(1).to_broadcast([P, a1 - a0, j1 - j0]), ALU.mult
            )
            queue.dma_start(out_v[:, a0:a1, j0:j1], res[:])

        pos = [sb([P, PACK * CH], F32, "pos%d" % c) for c in range(3)]
        z = [sb([P, PACK * CH], BF16, "z%d" % c) for c in range(4)]
        quant_w(woven_early[:], 0, HALF)
        nc.scalar.copy(w_codes[:, HALF:N], w_codes[:, 0:HALF])
        nc.scalar.copy(w_scales[:, HALF:N].bitcast(U32), w_scales[:, 0:HALF].bitcast(U32))
        warm = bank([WARM_M, N], "warm", "b6")
        for width in WARM_WIDTHS:
            nc.tensor.matmul_mx(
                out=warm[:, 0:width],
                lhsT=w_codes[:, 0:WARM_M].bitcast(FP8X4),
                lhsT_scale=w_scales[:, 0:WARM_M],
                rhs=w_codes[:, 0:width].bitcast(FP8X4),
                rhs_scale=w_scales[:, 0:width],
                start=True,
                stop=True,
            )
        first = [score(0, t, t + 1, tag) for t, tag in enumerate(("b0", "b1", "b2", "b6"))]
        second = [score(1, 0, 2, "b3"), score(1, 3, 4, "b5"), score(1, 2, 3, "b7")]
        for t in range(2):
            relu_scalar(pos[0], first[t], t, t + 1)
        third = [score(2, 0, 2, "b4"), score(2, 2, 4, "b0")]
        fourth = score(3, 0, 4, "b1")
        for t in range(2, PACK):
            relu_scalar(pos[0], first[t], t, t + 1)
        relu_scalar(pos[1], second[1], 3, 4)
        relu_vector_slots(pos[1], second[0], 0, 2)
        relu_vector_slots(pos[1], second[2], 2, 3)
        square(z[0], pos[0])
        square(z[1], pos[1])
        relu_vector_slots(pos[2], third[0], 0, 2)
        relu_vector_slots(pos[2], third[1], 2, 4)

        def values(chunks, a0, a1, tag):
            sums = bank([P, a1 - a0, len(chunks) * CH], "sums_%d_%d" % (chunks[0], a0), tag)
            for u, c in enumerate(chunks):
                for a in range(a0, a1):
                    value(sums[:, a - a0, u * CH : (u + 1) * CH], c, a)
            return sums

        quant_z(0, z[0])
        woven_late = sb([P, HALF, PACK], BF16, "woven_late", "pos0")
        nc.vector.tensor_copy(
            woven_late[:].rearrange("p m t -> p (m t)").bitcast(F32).rearrange("p (c i u) -> p c u i", i=2, u=2),
            cast_late[:].rearrange("p u m e -> p (u m e)").bitcast(F32).rearrange("p (u c i) -> p c u i", i=2, u=2),
        )
        quant_z(1, z[1])
        front = values((0, 1), 0, 2, "b6")
        quant_w(woven_late[:], HALF, N)
        back = values((0, 1), 2, 4, "b4")
        square(z[2], pos[2])
        pos.append(sb([P, PACK * CH], F32, "pos3", "pos1"))
        relu_scalar(pos[3], fourth, 0, 4)
        quant_z(2, z[2])
        whole = values((2,), 0, 4, "b0")
        finish(front, 0, 2, 0, 2 * CH, nc.sync)
        square(z[3], pos[3])
        finish(back, 2, 4, 0, 2 * CH, nc.sync)
        quant_z(3, z[3])
        last = [values((3,), 0, 2, "b5"), values((3,), 2, 4, "b2")]
        finish(whole, 0, 4, 2 * CH, 3 * CH, nc.scalar, "pos1")
        finish(last[0], 0, 2, 3 * CH, 4 * CH, nc.sync)
        finish(last[1], 2, 4, 3 * CH, 4 * CH, nc.scalar)
